import numpy as np
import ml_dtypes


def mxq(x, axis, fmt="e4m3"):
    dtype, down = {"e4m3": (ml_dtypes.float8_e4m3fn, 7), "e5m2": (ml_dtypes.float8_e5m2, 14)}[fmt]
    v = np.moveaxis(np.asarray(x, np.float32).astype(ml_dtypes.bfloat16).astype(np.float64), axis, -1)
    blocks = v.reshape(v.shape[:-1] + (-1, 32))
    amax = np.abs(blocks).max(-1, keepdims=True)
    byte = np.maximum(np.where(amax > 0, np.frexp(amax)[1] - 1 + 127, 0) - down, 1)
    scale = np.exp2(byte - 127.0)
    codes = (blocks / scale).astype(np.float32).astype(dtype).astype(np.float64)
    return np.moveaxis((codes * scale).reshape(v.shape), -1, axis)


WIDE = False


def mx_kscale(k):
    if not WIDE:
        return np.ones(k)
    levels = np.array([10, -10, 5, -5, 0])
    if k % 512:
        return np.exp2(np.random.permutation(np.resize(levels, k // 32))).repeat(32)
    a = np.empty((k // 512, 16))
    for p in range(k // 512):
        a[p, :8] = np.random.permutation(np.resize(levels, 8))
        for g in range(8):
            far = levels[np.abs(levels - a[p, g]) >= 10]
            a[p, g + 8] = far[np.random.randint(len(far))]
    return np.exp2(a.ravel()).repeat(32)


def f64(x):
    return np.asarray(x).astype(np.float64)


def striped(idx):
    return np.tile(idx.reshape(-1, 16).T, (8, 1)).astype(np.uint16)


def unstriped(offs):
    return offs[:16].T.reshape(-1).astype(np.int64)


E2M1 = np.array([0.0, 0.5, 1.0, 1.5, 2.0, 3.0, 4.0, 6.0, -0.0, -0.5, -1.0, -1.5, -2.0, -3.0, -4.0, -6.0])


def pack_weight(w, fmt):
    k, n = w.shape
    w = f64(np.asarray(w, np.float32).astype(ml_dtypes.bfloat16)).reshape(k // 32, 32, n)
    amax = np.abs(w).max(1)
    if fmt == "e4m3":
        byte = np.frexp(amax)[1] - 1 + 127 - 7
    else:
        mant, ex = np.frexp(amax / 6.0)
        byte = np.where(mant > 0.5, ex, ex - 1) + 127
    byte = np.clip(np.where(amax > 0, byte, 1), 1, 254)
    scaled = (w * np.exp2(127.0 - byte)[:, None, :]).reshape(k, n).astype(np.float32)
    by_word = np.ascontiguousarray(scaled.reshape(k // 512, 128, 4, n).transpose(0, 1, 3, 2))
    if fmt == "e4m3":
        words = by_word.astype(ml_dtypes.float8_e4m3fn).view(np.uint8)
    else:
        c = by_word.astype(ml_dtypes.float4_e2m1fn).view(np.uint8) & 0xF
        words = (c[..., 0::2] | (c[..., 1::2] << 4)).reshape(k // 512, 128, 2 * n)
    return np.ascontiguousarray(words), np.ascontiguousarray(byte.astype(np.uint8).reshape(k // 512, 16, n))


def unpack_weight(words, scales, fmt):
    g, _, n = scales.shape
    words = np.ascontiguousarray(words).reshape(g, 128, n, -1)
    if fmt == "e4m3":
        vals = words.view(ml_dtypes.float8_e4m3fn).astype(np.float64)
    else:
        nib = np.empty((g, 128, n, 4), np.uint8)
        nib[..., 0::2] = words & 0xF
        nib[..., 1::2] = words >> 4
        vals = E2M1[nib]
    vals = vals * np.repeat(np.exp2(scales.astype(np.float64) - 127.0), 8, axis=1)[..., None]
    return vals.transpose(0, 1, 3, 2).reshape(g * 512, n)


def silu(v):
    return v / (1.0 + np.exp(-np.maximum(v, -700.0)))


K, T, E, C, H, N, HOT = 512, 768, 9, 256, 512, 128, 3
TOP = 3


def by_expert(wq, xq):
    return np.concatenate([wq[e].T @ xq[:, e * C:(e + 1) * C] for e in range(E)], axis=1)


def setup_inputs():
    n = np.random.standard_normal
    s = mx_kscale(K)
    u = mx_kscale(H)
    deal = np.repeat(np.arange(E), C).reshape(TOP, T)[:, np.random.permutation(T)]
    deal = np.take_along_axis(deal, np.argsort(np.random.rand(TOP, T), axis=0), axis=0)
    for _ in range(8):
        s_, t_ = np.random.permutation(T).reshape(2, -1); r = np.random.randint(TOP, size=T // 2); x, y = deal[r, s_].copy(), deal[r, t_].copy()
        ok = ~((deal[:, s_] == y).any(0) | (deal[:, t_] == x).any(0)); deal[r[ok], s_[ok]] = y[ok]; deal[r[ok], t_[ok]] = x[ok]
    order = np.lexsort((np.random.rand(TOP * T), deal.reshape(-1)))
    slot_token = order % T; pos = np.empty(TOP * T, np.int64); pos[order] = np.arange(TOP * T); pos = pos.reshape(TOP, T)
    g = np.random.uniform(0.5, 1.5, (TOP, T)); g = g / g.sum(0)
    x = pack_weight(n((K, T)) * s[:, None], "e4m3")
    w1h = [pack_weight(m, "e4m3") for m in n((HOT, K, H)) / np.sqrt(K) / s[None, :, None] * u]
    w2h = [pack_weight(m, "e4m3") for m in n((HOT, H, N)) / np.sqrt(H) / u[None, :, None]]
    w1c = [pack_weight(m, "e2m1") for m in n((E - HOT, K, H)) / np.sqrt(K) / s[None, :, None] * u]
    w2c = [pack_weight(m, "e2m1") for m in n((E - HOT, H, N)) / np.sqrt(H) / u[None, :, None]]
    return {
        "x_words": x[0],
        "x_scales": x[1],
        "w1h_words": np.stack([m[0] for m in w1h]),
        "w1h_scales": np.stack([m[1] for m in w1h]),
        "w2h_words": np.stack([m[0] for m in w2h]),
        "w2h_scales": np.stack([m[1] for m in w2h]),
        "w1c_words": np.stack([m[0] for m in w1c]),
        "w1c_scales": np.stack([m[1] for m in w1c]),
        "w2c_words": np.stack([m[0] for m in w2c]),
        "w2c_scales": np.stack([m[1] for m in w2c]),
        "gate": np.stack([np.tile(r, (128, 1)) for r in g]).astype(np.float32),
        "offs": striped(slot_token),
        "pos1": striped(pos[0]),
        "pos2": striped(pos[1]),
        "pos3": striped(pos[2]),
    }


def reference(x_words, x_scales, w1h_words, w1h_scales, w2h_words, w2h_scales, w1c_words, w1c_scales, w2c_words, w2c_scales, gate, offs, pos1, pos2, pos3):
    w1h = np.stack([unpack_weight(w1h_words[e], w1h_scales[e], "e4m3") for e in range(HOT)])
    w2h = np.stack([unpack_weight(w2h_words[e], w2h_scales[e], "e4m3") for e in range(HOT)])
    w1c = np.stack([unpack_weight(w1c_words[e], w1c_scales[e], "e2m1") for e in range(E - HOT)])
    w2c = np.stack([unpack_weight(w2c_words[e], w2c_scales[e], "e2m1") for e in range(E - HOT)])
    idx = unstriped(offs)
    xq = unpack_weight(x_words, x_scales, "e4m3")[:, idx]
    w1 = [*w1h, *w1c]
    w2 = [*w2h, *w2c]
    h = silu(by_expert(w1, xq))
    y = by_expert(w2, mxq(h, 0, "e4m3"))
    out = sum(f64(gate[r, :1]) * y[:, unstriped(p)] for r, p in enumerate((pos1, pos2, pos3)))
    return out

@@ -1,0 +1,236 @@
+from contextlib import ExitStack
+
+import concourse.mybir as mybir
+from concourse.masks import make_identity
+
+K, T, E, C, H, N, HOT, TOP = 512, 768, 9, 256, 512, 128, 3, 3
+COLD = E - HOT
+S = E * C
+P = 128
+FLOPS = 2 * S * (K * H + H * N)
+
+F32 = mybir.dt.float32
+BF16 = mybir.dt.bfloat16
+I32 = mybir.dt.int32
+U32 = mybir.dt.uint32
+U16 = mybir.dt.uint16
+U8 = mybir.dt.uint8
+FP8X4 = mybir.dt.float8_e4m3fn_x4
+FP4X4 = mybir.dt.float4_e2m1fn_x4
+SILU = mybir.ActivationFunctionType.Silu
+MULT = mybir.AluOpType.mult
+ADD = mybir.AluOpType.add
+
+ORDER = list(range(HOT, E)) + list(range(HOT))
+Y_ON_VECTOR = 6
+BANKS = 5
+TOKEN_CHUNKS = [(0, 320), (320, 608), (608, 768)]
+
+
+def tile_moe_hot_mlp_silu_kernel(
+    tc, x_words, x_scales, w1h_words, w1h_scales, w2h_words, w2h_scales, w1c_words, w1c_scales,
+    w2c_words, w2c_scales, gate, offs, pos1, pos2, pos3, out,
+):
+    nc = tc.nc
+    with ExitStack() as ctx:
+        keep = ctx.enter_context(tc.tile_pool(name="keep", bufs=1))
+        ring = ctx.enter_context(tc.tile_pool(name="ring", bufs=4))
+        slots = ctx.enter_context(tc.tile_pool(name="slots", bufs=2))
+        psum_h = ctx.enter_context(tc.psum_pool(name="psum_h", bufs=3))
+        psum_t = ctx.enter_context(tc.psum_pool(name="psum_t", bufs=1))
+
+        offs_sb = keep.tile([P, S // 16], U16, name="offs_sb")
+        pos_sb = [keep.tile([P, T // 16], U16, name=f"pos_sb{r}") for r in range(TOP)]
+        xw = keep.tile([P, T], I32, name="xw", align_bytes=64)
+        xs = keep.tile([P, T], U8, name="xs", align_bytes=64)
+        w1c_first = keep.tile([P, 2 * H], U8, name="w1c_first", align_bytes=64)
+        w1c_rest = keep.tile([P, COLD - 1, 2 * H], U8, name="w1c_rest", align_bytes=64)
+        w1h_raw = keep.tile([P, HOT, H], I32, name="w1h_raw", align_bytes=64)
+        w1h = keep.tile([P, HOT, H], I32, name="w1h", align_bytes=64)
+        w2c = keep.tile([P, COLD, 2 * N], U8, name="w2c", align_bytes=64)
+        w2h = keep.tile([P, HOT, 4 * N], U8, name="w2h", align_bytes=64)
+        s1c_first = keep.tile([P, H], U8, name="s1c_first", align_bytes=64)
+        s1c_rest = keep.tile([P, COLD - 1, H], U8, name="s1c_rest", align_bytes=64)
+        s1h_raw = keep.tile([P, H], U8, name="s1h_raw", align_bytes=64)
+        s1h = keep.tile([P, H], U8, name="s1h", align_bytes=64)
+        s2c = keep.tile([P, COLD, N], U8, name="s2c", align_bytes=64)
+        s2h = keep.tile([P, HOT, N], U8, name="s2h", align_bytes=64)
+        gate_sb = keep.tile([P, TOP, T], F32, name="gate_sb")
+        y = keep.tile([P, S], F32, name="y")
+        ident = keep.tile([P, P], F32, name="ident")
+        warm = keep.tile([P, 8], F32, name="warm")
+        warm_out = keep.tile([P, 8], F32, name="warm_out")
+
+        nc.gpsimd.memset(warm[:], 0.0)
+        nc.scalar.activation(warm_out[:], warm[:], SILU)
+        for plane in (s1c_rest, s2c, s1h_raw, s2h):
+            nc.vector.memset(plane[:].bitcast(I32), 0)
+        make_identity(nc, ident[:])
+
+        def load_scales(plane, scales):
+            for q in range(4):
+                nc.sync.dma_start(
+                    plane[32 * q : 32 * q + 4].bitcast(I32),
+                    scales[:, 0, 4 * q : 4 * q + 4, :].rearrange("e b i -> b e i").bitcast(I32),
+                )
+
+        def load_scales_repeated(plane, rows):
+            words = rows.shape[1] // 4
+            for q in range(4):
+                nc.sync.dma_start(
+                    plane[32 * q : 32 * q + 32, :].bitcast(I32),
+                    rows[4 * q : 4 * q + 4, :].bitcast(I32).unsqueeze(0).broadcast_to([8, 4, words]),
+                )
+
+        nc.sync.dma_start(offs_sb[:], offs)
+        load_scales_repeated(xs, x_scales[0])
+        nc.sync.dma_start(xw[:], x_words[0].rearrange("p t d -> p (t d)").bitcast(I32))
+        nc.sync.dma_start(w1c_first[:].bitcast(I32), w1c_words[0, 0].bitcast(I32))
+        load_scales_repeated(s1c_first, w1c_scales[0, 0])
+        load_scales(s1c_rest, w1c_scales[1:])
+        nc.sync.dma_start(
+            w1c_rest[:].bitcast(I32), w1c_words[1:, 0].rearrange("f p b -> p f b").bitcast(I32)
+        )
+        nc.sync.dma_start(w2c[:].bitcast(I32), w2c_words[:, 0].rearrange("f p b -> p f b").bitcast(I32))
+        load_scales(s2c, w2c_scales)
+        nc.sync.dma_start(
+            w1h_raw[:], w1h_words[:, 0].rearrange("e p i d -> p e (i d)").bitcast(I32)
+        )
+        for q in range(4):
+            nc.sync.dma_start(
+                s1h_raw[32 * q : 32 * q + 4 * HOT, :].bitcast(I32),
+                w1h_scales[:, 0, 4 * q : 4 * q + 4, :].bitcast(I32),
+            )
+        nc.sync.dma_start(
+            w2h[:].bitcast(I32), w2h_words[:, 0].rearrange("e p n d -> p e (n d)").bitcast(I32)
+        )
+        load_scales(s2h, w2h_scales)
+        for r, pos in enumerate((pos1, pos2, pos3)):
+            nc.sync.dma_start(pos_sb[r][:], pos)
+        nc.sync.dma_start(gate_sb[:], gate.rearrange("r p t -> p r t"))
+
+        def first_matrix(e):
+            f = e - HOT
+            if f == 0:
+                return w1c_first[:].bitcast(FP4X4), s1c_first[:]
+            return w1c_rest[:, f - 1, :].bitcast(FP4X4), s1c_rest[:, f - 1, :]
+
+        def second_matrix(e):
+            if e < HOT:
+                return w2h[:, e, :].bitcast(FP8X4), s2h[:, e, :]
+            return w2c[:, e - HOT, :].bitcast(FP4X4), s2c[:, e - HOT, :]
+
+        def second_layer(group, step, first, width, w2, w2_scale, h_words, h_scales):
+            y_ps = psum_t.tile([P, width], F32, name="y_ps", tag=f"bank{(group + 1) % BANKS}")
+            nc.tensor.matmul_mx(
+                y_ps[:], lhsT=w2, lhsT_scale=w2_scale,
+                rhs=h_words[:].bitcast(FP8X4), rhs_scale=h_scales[:], start=True, stop=True,
+            )
+            if step < Y_ON_VECTOR:
+                nc.vector.tensor_copy(y[:, first : first + width], y_ps[:])
+            else:
+                nc.scalar.copy(y[:, first : first + width], y_ps[:])
+
+        def hidden_cold(group, e, blocks, slot_words, slot_scales, grouped):
+            w1, w1_scale = first_matrix(e)
+            turned = psum_t.tile([P, len(blocks), 2, P], F32, name="turned", tag=f"bank{group % BANKS}")
+            hs = []
+            for b in blocks:
+                pre = psum_h.tile([P, H], F32, name="pre")
+                nc.tensor.matmul_mx(
+                    pre[:],
+                    lhsT=slot_words[:, b * P : (b + 1) * P].bitcast(FP8X4),
+                    lhsT_scale=slot_scales[:, b * P : (b + 1) * P],
+                    rhs=w1, rhs_scale=w1_scale, start=True, stop=True,
+                )
+                h = ring.tile([P, H], BF16, name="h")
+                nc.scalar.activation(
+                    h[:].rearrange("s (u p d) -> s u p d", u=2, d=2),
+                    pre[:].rearrange("s (p u d) -> s u p d", u=2, d=2),
+                    SILU,
+                )
+                hs.append(h)
+            for j, h in enumerate(hs):
+                for u in range(2):
+                    nc.tensor.transpose(
+                        turned[:, j, u, :], h[:].bitcast(F32)[:, u * P : (u + 1) * P], ident[:]
+                    )
+            nc.scalar.copy(
+                grouped[:].bitcast(F32).rearrange("p (b s u) -> p b s u", s=P, u=2),
+                turned[:].rearrange("p b u s -> p b s u"),
+            )
+
+        def hidden_hot(e, blocks, slot_words, slot_scales, grouped):
+            for j, b in enumerate(blocks):
+                pre = psum_h.tile([P, H], F32, name="pre")
+                for t in range(4):
+                    nc.tensor.matmul_mx(
+                        pre[:, t * P : (t + 1) * P],
+                        lhsT=w1h[:, e, t * P : (t + 1) * P].bitcast(FP8X4),
+                        lhsT_scale=s1h[4 * e :, t * P : (t + 1) * P],
+                        rhs=slot_words[:, b * P : (b + 1) * P].bitcast(FP8X4),
+                        rhs_scale=slot_scales[:, b * P : (b + 1) * P],
+                        start=True, stop=True,
+                    )
+                nc.scalar.activation(
+                    grouped[:, j * H : (j + 1) * H].rearrange("p (s t) -> p s t", t=4),
+                    pre[:].rearrange("p (t s) -> p s t", t=4),
+                    SILU,
+                )
+
+        def permute_columns(dst, src, line):
+            nc.vector.tensor_copy(
+                dst.rearrange("p (t c i) -> p c t i", t=4, i=line),
+                src.rearrange("p (c i t) -> p c t i", t=4, i=line),
+            )
+
+        group = 0
+        waiting = None
+        for step, e in enumerate(ORDER):
+            if e == 0:
+                permute_columns(s1h[:], s1h_raw[:], 16)
+            if e < HOT:
+                permute_columns(w1h[:, e, :], w1h_raw[:, e, :], 4)
+            slot_words = slots.tile([P, C], U32, name="slot_words", align_bytes=64)
+            slot_scales = slots.tile([P, C], U8, name="slot_scales", align_bytes=64)
+            col = e * C // 16
+            nc.vector.tensor_copy(slot_scales[:], xs[:].indirect(offs_sb[:, col : col + C // 16]))
+            pieces = 2 if step == 0 else 1
+            for a in range(pieces):
+                w = C // pieces
+                nc.vector.tensor_copy(
+                    slot_words[:, a * w : (a + 1) * w],
+                    xw[:].bitcast(U32).indirect(offs_sb[:, col + a * w // 16 : col + (a + 1) * w // 16]),
+                )
+
+            w2, w2_scale = second_matrix(e)
+            groups = [[0], [1]] if step == E - 1 else [[0, 1]]
+            for blocks in groups:
+                width = P * len(blocks)
+                grouped = ring.tile([P, 4 * width], BF16, name="grouped", align_bytes=64)
+                if e < HOT:
+                    hidden_hot(e, blocks, slot_words, slot_scales, grouped)
+                else:
+                    hidden_cold(group, e, blocks, slot_words, slot_scales, grouped)
+                h_words = ring.tile([P, width], U32, name="h_words", align_bytes=64)
+                h_scales = ring.tile([P, width], U8, name="h_scales", align_bytes=64)
+                nc.vector.quantize_mx(h_words[:].bitcast(FP8X4), h_scales[:], grouped[:])
+                if waiting is not None:
+                    second_layer(*waiting)
+                waiting = (group, step, e * C + blocks[0] * P, width, w2, w2_scale, h_words, h_scales)
+                group += 1
+        second_layer(*waiting)
+
+        for lo, hi in TOKEN_CHUNKS:
+            parts = []
+            for r in range(TOP):
+                part = keep.tile([P, hi - lo], F32, name=f"part{r}_{lo}")
+                nc.vector.tensor_tensor(
+                    part[:], y[:].indirect(pos_sb[r][:, lo // 16 : hi // 16]), gate_sb[:, r, lo:hi], MULT
+                )
+                parts.append(part)
+            pair = keep.tile([P, hi - lo], F32, name=f"pair{lo}")
+            total = keep.tile([P, hi - lo], F32, name=f"total{lo}")
+            nc.vector.tensor_tensor(pair[:], parts[0][:], parts[1][:], ADD)
+            nc.vector.tensor_tensor(total[:], pair[:], parts[2][:], ADD)
+            nc.sync.dma_start(out[:, lo:hi], total[:])

@@ -22,9 +22,11 @@ MULT = mybir.AluOpType.mult
 ADD = mybir.AluOpType.add
 
 ORDER = list(range(HOT, E)) + list(range(HOT))
-Y_ON_VECTOR = 6
+Y_ON_VECTOR = (1, 2, 4, 5, 7, 10,)
+TURN_ON_VECTOR = ()
 BANKS = 5
-TOKEN_CHUNKS = [(0, 320), (320, 608), (608, 768)]
+TOKEN_CHUNKS = [(0, 256), (256, 512), (512, 672), (672, 768)]
+SUMMED_IN_PSUM = 2
 
 
 def tile_moe_hot_mlp_silu_kernel(
@@ -34,7 +36,7 @@ def tile_moe_hot_mlp_silu_kernel(
     nc = tc.nc
     with ExitStack() as ctx:
         keep = ctx.enter_context(tc.tile_pool(name="keep", bufs=1))
-        ring = ctx.enter_context(tc.tile_pool(name="ring", bufs=4))
+        ring = ctx.enter_context(tc.tile_pool(name="ring", bufs=5))
         slots = ctx.enter_context(tc.tile_pool(name="slots", bufs=2))
         psum_h = ctx.enter_context(tc.psum_pool(name="psum_h", bufs=3))
         psum_t = ctx.enter_context(tc.psum_pool(name="psum_t", bufs=1))
@@ -44,15 +46,13 @@ def tile_moe_hot_mlp_silu_kernel(
         xw = keep.tile([P, T], I32, name="xw", align_bytes=64)
         xs = keep.tile([P, T], U8, name="xs", align_bytes=64)
         w1c_first = keep.tile([P, 2 * H], U8, name="w1c_first", align_bytes=64)
-        w1c_rest = keep.tile([P, COLD - 1, 2 * H], U8, name="w1c_rest", align_bytes=64)
+        w1c_mid = keep.tile([P, 3, 2 * H], U8, name="w1c_mid", align_bytes=64)
+        w1c_last = keep.tile([P, 2, 2 * H], U8, name="w1c_last", align_bytes=64)
         w1h_raw = keep.tile([P, HOT, H], I32, name="w1h_raw", align_bytes=64)
-        w1h = keep.tile([P, HOT, H], I32, name="w1h", align_bytes=64)
         w2c = keep.tile([P, COLD, 2 * N], U8, name="w2c", align_bytes=64)
         w2h = keep.tile([P, HOT, 4 * N], U8, name="w2h", align_bytes=64)
-        s1c_first = keep.tile([P, H], U8, name="s1c_first", align_bytes=64)
-        s1c_rest = keep.tile([P, COLD - 1, H], U8, name="s1c_rest", align_bytes=64)
+        s1c = keep.tile([P, COLD, H], U8, name="s1c", align_bytes=64)
         s1h_raw = keep.tile([P, H], U8, name="s1h_raw", align_bytes=64)
-        s1h = keep.tile([P, H], U8, name="s1h", align_bytes=64)
         s2c = keep.tile([P, COLD, N], U8, name="s2c", align_bytes=64)
         s2h = keep.tile([P, HOT, N], U8, name="s2h", align_bytes=64)
         gate_sb = keep.tile([P, TOP, T], F32, name="gate_sb")
@@ -61,15 +61,17 @@ def tile_moe_hot_mlp_silu_kernel(
         warm = keep.tile([P, 8], F32, name="warm")
         warm_out = keep.tile([P, 8], F32, name="warm_out")
 
-        nc.gpsimd.memset(warm[:], 0.0)
+        nc.vector.memset(warm[:], 0.0)
         nc.scalar.activation(warm_out[:], warm[:], SILU)
-        for plane in (s1c_rest, s2c, s1h_raw, s2h):
-            nc.vector.memset(plane[:].bitcast(I32), 0)
+        nc.vector.memset(s1c[:].bitcast(I32), 0)
+        nc.vector.memset(s2c[:].bitcast(I32), 0)
+        nc.vector.memset(s1h_raw[:].bitcast(I32), 0)
+        nc.vector.memset(s2h[:].bitcast(I32), 0)
         make_identity(nc, ident[:])
 
-        def load_scales(plane, scales):
+        def load_scales(plane, scales, queue):
             for q in range(4):
-                nc.sync.dma_start(
+                queue.dma_start(
                     plane[32 * q : 32 * q + 4].bitcast(I32),
                     scales[:, 0, 4 * q : 4 * q + 4, :].rearrange("e b i -> b e i").bitcast(I32),
                 )
@@ -86,34 +88,29 @@ def tile_moe_hot_mlp_silu_kernel(
         load_scales_repeated(xs, x_scales[0])
         nc.sync.dma_start(xw[:], x_words[0].rearrange("p t d -> p (t d)").bitcast(I32))
         nc.sync.dma_start(w1c_first[:].bitcast(I32), w1c_words[0, 0].bitcast(I32))
-        load_scales_repeated(s1c_first, w1c_scales[0, 0])
-        load_scales(s1c_rest, w1c_scales[1:])
-        nc.sync.dma_start(
-            w1c_rest[:].bitcast(I32), w1c_words[1:, 0].rearrange("f p b -> p f b").bitcast(I32)
-        )
-        nc.sync.dma_start(w2c[:].bitcast(I32), w2c_words[:, 0].rearrange("f p b -> p f b").bitcast(I32))
-        load_scales(s2c, w2c_scales)
-        nc.sync.dma_start(
-            w1h_raw[:], w1h_words[:, 0].rearrange("e p i d -> p e (i d)").bitcast(I32)
-        )
+        nc.sync.dma_start(w1c_mid[:].bitcast(I32), w1c_words[1:4, 0].rearrange("f p b -> p f b").bitcast(I32))
+        load_scales(s1c, w1c_scales, nc.sync)
+        nc.sync.dma_start(w2h[:].bitcast(I32), w2h_words[:, 0].rearrange("e p n d -> p e (n d)").bitcast(I32))
+        load_scales(s2c, w2c_scales, nc.sync)
+        nc.sync.dma_start(w1c_last[:].bitcast(I32), w1c_words[4:, 0].rearrange("f p b -> p f b").bitcast(I32))
+        nc.sync.dma_start(w1h_raw[:], w1h_words[:, 0].rearrange("e p i d -> p e (i d)").bitcast(I32))
         for q in range(4):
             nc.sync.dma_start(
                 s1h_raw[32 * q : 32 * q + 4 * HOT, :].bitcast(I32),
                 w1h_scales[:, 0, 4 * q : 4 * q + 4, :].bitcast(I32),
             )
-        nc.sync.dma_start(
-            w2h[:].bitcast(I32), w2h_words[:, 0].rearrange("e p n d -> p e (n d)").bitcast(I32)
-        )
-        load_scales(s2h, w2h_scales)
         for r, pos in enumerate((pos1, pos2, pos3)):
             nc.sync.dma_start(pos_sb[r][:], pos)
+        nc.sync.dma_start(w2c[:].bitcast(I32), w2c_words[:, 0].rearrange("f p b -> p f b").bitcast(I32))
         nc.sync.dma_start(gate_sb[:], gate.rearrange("r p t -> p r t"))
+        load_scales(s2h, w2h_scales, nc.sync)
 
         def first_matrix(e):
             f = e - HOT
             if f == 0:
-                return w1c_first[:].bitcast(FP4X4), s1c_first[:]
-            return w1c_rest[:, f - 1, :].bitcast(FP4X4), s1c_rest[:, f - 1, :]
+                return w1c_first[:].bitcast(FP4X4), s1c[:, 0, :]
+            words = w1c_mid[:, f - 1, :] if f < 4 else w1c_last[:, f - 4, :]
+            return words.bitcast(FP4X4), s1c[:, f, :]
 
         def second_matrix(e):
             if e < HOT:
@@ -126,7 +123,7 @@ def tile_moe_hot_mlp_silu_kernel(
                 y_ps[:], lhsT=w2, lhsT_scale=w2_scale,
                 rhs=h_words[:].bitcast(FP8X4), rhs_scale=h_scales[:], start=True, stop=True,
             )
-            if step < Y_ON_VECTOR:
+            if group in Y_ON_VECTOR:
                 nc.vector.tensor_copy(y[:, first : first + width], y_ps[:])
             else:
                 nc.scalar.copy(y[:, first : first + width], y_ps[:])
@@ -155,12 +152,12 @@ def tile_moe_hot_mlp_silu_kernel(
                     nc.tensor.transpose(
                         turned[:, j, u, :], h[:].bitcast(F32)[:, u * P : (u + 1) * P], ident[:]
                     )
-            nc.scalar.copy(
+            (nc.vector.tensor_copy if group in TURN_ON_VECTOR else nc.scalar.copy)(
                 grouped[:].bitcast(F32).rearrange("p (b s u) -> p b s u", s=P, u=2),
                 turned[:].rearrange("p b u s -> p b s u"),
             )
 
-        def hidden_hot(e, blocks, slot_words, slot_scales, grouped):
+        def hidden_hot(e, blocks, slot_words, slot_scales, grouped, w1h, s1h):
             for j, b in enumerate(blocks):
                 pre = psum_h.tile([P, H], F32, name="pre")
                 for t in range(4):
@@ -179,7 +176,7 @@ def tile_moe_hot_mlp_silu_kernel(
                 )
 
         def permute_columns(dst, src, line):
-            nc.vector.tensor_copy(
+            nc.gpsimd.tensor_copy(
                 dst.rearrange("p (t c i) -> p c t i", t=4, i=line),
                 src.rearrange("p (c i t) -> p c t i", t=4, i=line),
             )
@@ -187,29 +184,30 @@ def tile_moe_hot_mlp_silu_kernel(
         group = 0
         waiting = None
         for step, e in enumerate(ORDER):
-            if e == 0:
-                permute_columns(s1h[:], s1h_raw[:], 16)
-            if e < HOT:
-                permute_columns(w1h[:, e, :], w1h_raw[:, e, :], 4)
+            if step == 1:
+                hot_first = keep.tile([P, HOT * 4 * H + H], U8, name="hot_first", align_bytes=64)
+                w1h = hot_first[:, : HOT * 4 * H].bitcast(I32).rearrange("p (e i) -> p e i", e=HOT)
+                s1h = hot_first[:, HOT * 4 * H :]
+                for a in range(HOT):
+                    permute_columns(w1h[:, a, :], w1h_raw[:, a, :], 4)
+                permute_columns(s1h, s1h_raw[:], 16)
             slot_words = slots.tile([P, C], U32, name="slot_words", align_bytes=64)
             slot_scales = slots.tile([P, C], U8, name="slot_scales", align_bytes=64)
             col = e * C // 16
-            nc.vector.tensor_copy(slot_scales[:], xs[:].indirect(offs_sb[:, col : col + C // 16]))
-            pieces = 2 if step == 0 else 1
+            pieces = 2 if step in (0, 8, ) else 1
             for a in range(pieces):
                 w = C // pieces
-                nc.vector.tensor_copy(
-                    slot_words[:, a * w : (a + 1) * w],
-                    xw[:].bitcast(U32).indirect(offs_sb[:, col + a * w // 16 : col + (a + 1) * w // 16]),
-                )
+                piece = offs_sb[:, col + a * w // 16 : col + (a + 1) * w // 16]
+                nc.vector.tensor_copy(slot_scales[:, a * w : (a + 1) * w], xs[:].indirect(piece))
+                nc.vector.tensor_copy(slot_words[:, a * w : (a + 1) * w], xw[:].bitcast(U32).indirect(piece))
 
             w2, w2_scale = second_matrix(e)
-            groups = [[0], [1]] if step == E - 1 else [[0, 1]]
+            groups = [[0], [1]] if step in (0, 8, ) else [[0, 1]]
             for blocks in groups:
                 width = P * len(blocks)
                 grouped = ring.tile([P, 4 * width], BF16, name="grouped", align_bytes=64)
                 if e < HOT:
-                    hidden_hot(e, blocks, slot_words, slot_scales, grouped)
+                    hidden_hot(e, blocks, slot_words, slot_scales, grouped, w1h, s1h)
                 else:
                     hidden_cold(group, e, blocks, slot_words, slot_scales, grouped)
                 h_words = ring.tile([P, width], U32, name="h_words", align_bytes=64)
@@ -221,16 +219,34 @@ def tile_moe_hot_mlp_silu_kernel(
                 group += 1
         second_layer(*waiting)
 
-        for lo, hi in TOKEN_CHUNKS:
+        for chunk, (lo, hi) in enumerate(TOKEN_CHUNKS):
+            width = hi - lo
             parts = []
             for r in range(TOP):
-                part = keep.tile([P, hi - lo], F32, name=f"part{r}_{lo}")
+                part = keep.tile([P, width], F32, name=f"part{r}_{lo}")
                 nc.vector.tensor_tensor(
                     part[:], y[:].indirect(pos_sb[r][:, lo // 16 : hi // 16]), gate_sb[:, r, lo:hi], MULT
                 )
                 parts.append(part)
-            pair = keep.tile([P, hi - lo], F32, name=f"pair{lo}")
-            total = keep.tile([P, hi - lo], F32, name=f"total{lo}")
-            nc.vector.tensor_tensor(pair[:], parts[0][:], parts[1][:], ADD)
-            nc.vector.tensor_tensor(total[:], pair[:], parts[2][:], ADD)
-            nc.sync.dma_start(out[:, lo:hi], total[:])
+            total = keep.tile([P, width], F32, name=f"total{lo}")
+            if chunk < SUMMED_IN_PSUM:
+                sum_sb = keep.tile([P, width], F32, name=f"sum_sb{lo}")
+                for b in range(width // P):
+                    cols = slice(b * P, (b + 1) * P)
+                    sum_ps = psum_t.tile([P, P], F32, name="sum_ps", tag=f"bank{(lo // P + b + 1) % BANKS}")
+                    for r in range(TOP):
+                        nc.tensor.matmul(
+                            sum_ps[:], parts[r][:, cols], ident[:],
+                            start=(r == 0), stop=(r == TOP - 1), is_transpose=True,
+                        )
+                    nc.scalar.copy(sum_sb[:, cols], sum_ps[:])
+                back_ps = psum_h.tile([P, width], F32, name="pre")
+                for b in range(width // P):
+                    cols = slice(b * P, (b + 1) * P)
+                    nc.tensor.transpose(back_ps[:, cols], sum_sb[:, cols], ident[:])
+                nc.scalar.copy(total[:], back_ps[:])
+            else:
+                pair = keep.tile([P, width], F32, name=f"pair{lo}")
+                nc.vector.tensor_tensor(pair[:], parts[0][:], parts[1][:], ADD)
+                nc.vector.tensor_tensor(total[:], pair[:], parts[2][:], ADD)
+            (nc.scalar if chunk < SUMMED_IN_PSUM else nc.sync).dma_start(out[:, lo:hi], total[:])

@@ -22,10 +22,10 @@ MULT = mybir.AluOpType.mult
 ADD = mybir.AluOpType.add
 
 ORDER = list(range(HOT, E)) + list(range(HOT))
-Y_ON_VECTOR = (1, 2, 4, 5, 7, 10,)
+Y_ON_VECTOR = (0, 1, 6, 7, 8,)
 TURN_ON_VECTOR = ()
 BANKS = 5
-TOKEN_CHUNKS = [(0, 256), (256, 512), (512, 672), (672, 768)]
+TOKEN_CHUNKS = [(0, 384), (384, 512), (512, 640), (640, 768)]
 SUMMED_IN_PSUM = 2
 
 
@@ -36,8 +36,8 @@ def tile_moe_hot_mlp_silu_kernel(
     nc = tc.nc
     with ExitStack() as ctx:
         keep = ctx.enter_context(tc.tile_pool(name="keep", bufs=1))
-        ring = ctx.enter_context(tc.tile_pool(name="ring", bufs=5))
-        slots = ctx.enter_context(tc.tile_pool(name="slots", bufs=2))
+        ring = ctx.enter_context(tc.tile_pool(name="ring", bufs=7))
+        slots = ctx.enter_context(tc.tile_pool(name="slots", bufs=3))
         psum_h = ctx.enter_context(tc.psum_pool(name="psum_h", bufs=3))
         psum_t = ctx.enter_context(tc.psum_pool(name="psum_t", bufs=1))
 
@@ -45,13 +45,14 @@ def tile_moe_hot_mlp_silu_kernel(
         pos_sb = [keep.tile([P, T // 16], U16, name=f"pos_sb{r}") for r in range(TOP)]
         xw = keep.tile([P, T], I32, name="xw", align_bytes=64)
         xs = keep.tile([P, T], U8, name="xs", align_bytes=64)
-        w1c_first = keep.tile([P, 2 * H], U8, name="w1c_first", align_bytes=64)
-        w1c_mid = keep.tile([P, 3, 2 * H], U8, name="w1c_mid", align_bytes=64)
+        w1c_first = keep.tile([P, 2, 2 * H], U8, name="w1c_first", align_bytes=64)
+        w1c_mid = keep.tile([P, 2, 2 * H], U8, name="w1c_mid", align_bytes=64)
         w1c_last = keep.tile([P, 2, 2 * H], U8, name="w1c_last", align_bytes=64)
         w1h_raw = keep.tile([P, HOT, H], I32, name="w1h_raw", align_bytes=64)
         w2c = keep.tile([P, COLD, 2 * N], U8, name="w2c", align_bytes=64)
         w2h = keep.tile([P, HOT, 4 * N], U8, name="w2h", align_bytes=64)
-        s1c = keep.tile([P, COLD, H], U8, name="s1c", align_bytes=64)
+        s1c_first = keep.tile([P, 2, H], U8, name="s1c_first", align_bytes=64)
+        s1c_rest = keep.tile([P, COLD - 2, H], U8, name="s1c_rest", align_bytes=64)
         s1h_raw = keep.tile([P, H], U8, name="s1h_raw", align_bytes=64)
         s2c = keep.tile([P, COLD, N], U8, name="s2c", align_bytes=64)
         s2h = keep.tile([P, HOT, N], U8, name="s2h", align_bytes=64)
@@ -63,7 +64,8 @@ def tile_moe_hot_mlp_silu_kernel(
 
         nc.vector.memset(warm[:], 0.0)
         nc.scalar.activation(warm_out[:], warm[:], SILU)
-        nc.vector.memset(s1c[:].bitcast(I32), 0)
+        nc.vector.memset(s1c_first[:].bitcast(I32), 0)
+        nc.vector.memset(s1c_rest[:].bitcast(I32), 0)
         nc.vector.memset(s2c[:].bitcast(I32), 0)
         nc.vector.memset(s1h_raw[:].bitcast(I32), 0)
         nc.vector.memset(s2h[:].bitcast(I32), 0)
@@ -84,33 +86,33 @@ def tile_moe_hot_mlp_silu_kernel(
                     rows[4 * q : 4 * q + 4, :].bitcast(I32).unsqueeze(0).broadcast_to([8, 4, words]),
                 )
 
-        nc.sync.dma_start(offs_sb[:], offs)
         load_scales_repeated(xs, x_scales[0])
+        nc.sync.dma_start(offs_sb[:], offs)
         nc.sync.dma_start(xw[:], x_words[0].rearrange("p t d -> p (t d)").bitcast(I32))
-        nc.sync.dma_start(w1c_first[:].bitcast(I32), w1c_words[0, 0].bitcast(I32))
-        nc.sync.dma_start(w1c_mid[:].bitcast(I32), w1c_words[1:4, 0].rearrange("f p b -> p f b").bitcast(I32))
-        load_scales(s1c, w1c_scales, nc.sync)
-        nc.sync.dma_start(w2h[:].bitcast(I32), w2h_words[:, 0].rearrange("e p n d -> p e (n d)").bitcast(I32))
-        load_scales(s2c, w2c_scales, nc.sync)
-        nc.sync.dma_start(w1c_last[:].bitcast(I32), w1c_words[4:, 0].rearrange("f p b -> p f b").bitcast(I32))
+        nc.sync.dma_start(w1c_first[:].bitcast(I32), w1c_words[:2, 0].rearrange("f p b -> p f b").bitcast(I32))
+        load_scales(s1c_first, w1c_scales[:2], nc.sync)
         nc.sync.dma_start(w1h_raw[:], w1h_words[:, 0].rearrange("e p i d -> p e (i d)").bitcast(I32))
+        nc.sync.dma_start(w1c_mid[:].bitcast(I32), w1c_words[2:4, 0].rearrange("f p b -> p f b").bitcast(I32))
+        nc.sync.dma_start(w1c_last[:].bitcast(I32), w1c_words[4:, 0].rearrange("f p b -> p f b").bitcast(I32))
+        load_scales(s1c_rest, w1c_scales[2:], nc.sync)
         for q in range(4):
             nc.sync.dma_start(
                 s1h_raw[32 * q : 32 * q + 4 * HOT, :].bitcast(I32),
                 w1h_scales[:, 0, 4 * q : 4 * q + 4, :].bitcast(I32),
             )
+        nc.sync.dma_start(w2h[:].bitcast(I32), w2h_words[:, 0].rearrange("e p n d -> p e (n d)").bitcast(I32))
+        nc.sync.dma_start(w2c[:].bitcast(I32), w2c_words[:, 0].rearrange("f p b -> p f b").bitcast(I32))
+        load_scales(s2h, w2h_scales, nc.sync)
+        nc.sync.dma_start(gate_sb[:], gate.rearrange("r p t -> p r t"))
         for r, pos in enumerate((pos1, pos2, pos3)):
             nc.sync.dma_start(pos_sb[r][:], pos)
-        nc.sync.dma_start(w2c[:].bitcast(I32), w2c_words[:, 0].rearrange("f p b -> p f b").bitcast(I32))
-        nc.sync.dma_start(gate_sb[:], gate.rearrange("r p t -> p r t"))
-        load_scales(s2h, w2h_scales, nc.sync)
+        load_scales(s2c, w2c_scales, nc.sync)
 
         def first_matrix(e):
             f = e - HOT
-            if f == 0:
-                return w1c_first[:].bitcast(FP4X4), s1c[:, 0, :]
-            words = w1c_mid[:, f - 1, :] if f < 4 else w1c_last[:, f - 4, :]
-            return words.bitcast(FP4X4), s1c[:, f, :]
+            words = (w1c_first, w1c_mid, w1c_last)[f // 2][:, f % 2, :]
+            scales = s1c_first[:, f, :] if f < 2 else s1c_rest[:, f - 2, :]
+            return words.bitcast(FP4X4), scales
 
         def second_matrix(e):
             if e < HOT:
@@ -176,7 +178,7 @@ def tile_moe_hot_mlp_silu_kernel(
                 )
 
         def permute_columns(dst, src, line):
-            nc.gpsimd.tensor_copy(
+            nc.vector.tensor_copy(
                 dst.rearrange("p (t c i) -> p c t i", t=4, i=line),
                 src.rearrange("p (c i t) -> p c t i", t=4, i=line),
             )
@@ -184,15 +186,15 @@ def tile_moe_hot_mlp_silu_kernel(
         group = 0
         waiting = None
         for step, e in enumerate(ORDER):
-            if step == 1:
+            if step == 4:
                 hot_first = keep.tile([P, HOT * 4 * H + H], U8, name="hot_first", align_bytes=64)
                 w1h = hot_first[:, : HOT * 4 * H].bitcast(I32).rearrange("p (e i) -> p e i", e=HOT)
                 s1h = hot_first[:, HOT * 4 * H :]
+                permute_columns(s1h, s1h_raw[:], 16)
                 for a in range(HOT):
                     permute_columns(w1h[:, a, :], w1h_raw[:, a, :], 4)
-                permute_columns(s1h, s1h_raw[:], 16)
             slot_words = slots.tile([P, C], U32, name="slot_words", align_bytes=64)
-            slot_scales = slots.tile([P, C], U8, name="slot_scales", align_bytes=64)
+            slot_scales = slots.tile([P, C], U8, name="slot_scales", align_bytes=64, bufs=2)
             col = e * C // 16
             pieces = 2 if step in (0, 8, ) else 1
             for a in range(pieces):
@@ -202,7 +204,7 @@ def tile_moe_hot_mlp_silu_kernel(
                 nc.vector.tensor_copy(slot_words[:, a * w : (a + 1) * w], xw[:].bitcast(U32).indirect(piece))
 
             w2, w2_scale = second_matrix(e)
-            groups = [[0], [1]] if step in (0, 8, ) else [[0, 1]]
+            groups = [[0], [1]] if step in () else [[0, 1]]
             for blocks in groups:
                 width = P * len(blocks)
                 grouped = ring.tile([P, 4 * width], BF16, name="grouped", align_bytes=64)

@@ -6,8 +6,13 @@ from concourse.masks import make_identity
 K, T, E, C, H, N, HOT, TOP = 512, 768, 9, 256, 512, 128, 3, 3
 COLD = E - HOT
 S = E * C
-P = 128
 FLOPS = 2 * S * (K * H + H * N)
+
+P = 128
+PACK = 4
+QUADRANTS = 4
+LIST_ROWS = 16
+BLOCKS = C // P
 
 F32 = mybir.dt.float32
 BF16 = mybir.dt.bfloat16
@@ -22,9 +27,14 @@ MULT = mybir.AluOpType.mult
 ADD = mybir.AluOpType.add
 
 ORDER = list(range(HOT, E)) + list(range(HOT))
-Y_ON_VECTOR = (0, 1, 6, 7, 8,)
-TURN_ON_VECTOR = ()
-BANKS = 5
+WORD_GATHERS = [1, 2, 3, 2, 2, 2, 2, 4]
+SCALE_GATHERS = [2, 2, 1, 3, 4, 4, 2]
+WORD_TILES, SCALE_TILES = 4, 3
+TURNED_ON_VECTOR = (5,)
+RESULT_ON_VECTOR = (1, 7,)
+GROUPS = [(0, 1), (2, 3), (4, 5), (6, 7), (8,)]
+FIRST_BANKS = 3
+SHARED_BANKS = 5
 TOKEN_CHUNKS = [(0, 384), (384, 512), (512, 640), (640, 768)]
 SUMMED_IN_PSUM = 2
 
@@ -36,21 +46,21 @@ def tile_moe_hot_mlp_silu_kernel(
     nc = tc.nc
     with ExitStack() as ctx:
         keep = ctx.enter_context(tc.tile_pool(name="keep", bufs=1))
-        ring = ctx.enter_context(tc.tile_pool(name="ring", bufs=7))
-        slots = ctx.enter_context(tc.tile_pool(name="slots", bufs=3))
-        psum_h = ctx.enter_context(tc.psum_pool(name="psum_h", bufs=3))
-        psum_t = ctx.enter_context(tc.psum_pool(name="psum_t", bufs=1))
+        ring = ctx.enter_context(tc.tile_pool(name="ring", bufs=5))
+        gathered = ctx.enter_context(tc.tile_pool(name="gathered", bufs=WORD_TILES))
+        psum_first = ctx.enter_context(tc.psum_pool(name="psum_first", bufs=FIRST_BANKS))
+        psum_shared = ctx.enter_context(tc.psum_pool(name="psum_shared", bufs=1))
 
-        offs_sb = keep.tile([P, S // 16], U16, name="offs_sb")
-        pos_sb = [keep.tile([P, T // 16], U16, name=f"pos_sb{r}") for r in range(TOP)]
-        xw = keep.tile([P, T], I32, name="xw", align_bytes=64)
-        xs = keep.tile([P, T], U8, name="xs", align_bytes=64)
-        w1c_first = keep.tile([P, 2, 2 * H], U8, name="w1c_first", align_bytes=64)
-        w1c_mid = keep.tile([P, 2, 2 * H], U8, name="w1c_mid", align_bytes=64)
-        w1c_last = keep.tile([P, 2, 2 * H], U8, name="w1c_last", align_bytes=64)
+        offs_sb = keep.tile([P, S // LIST_ROWS], U16, name="offs_sb")
+        pos_sb = [keep.tile([P, T // LIST_ROWS], U16, name=f"pos_sb{r}") for r in range(TOP)]
+        token_words = keep.tile([P, T], I32, name="token_words", align_bytes=64)
+        token_scales = keep.tile([P, T], U8, name="token_scales", align_bytes=64)
+        w1c = [
+            keep.tile([P, 2, 2 * H], U8, name=f"w1c{a}", tag=f"w1c{a}", align_bytes=64) for a in range(COLD // 2)
+        ]
         w1h_raw = keep.tile([P, HOT, H], I32, name="w1h_raw", align_bytes=64)
         w2c = keep.tile([P, COLD, 2 * N], U8, name="w2c", align_bytes=64)
-        w2h = keep.tile([P, HOT, 4 * N], U8, name="w2h", align_bytes=64)
+        w2h = keep.tile([P, HOT, PACK * N], U8, name="w2h", align_bytes=64)
         s1c_first = keep.tile([P, 2, H], U8, name="s1c_first", align_bytes=64)
         s1c_rest = keep.tile([P, COLD - 2, H], U8, name="s1c_rest", align_bytes=64)
         s1h_raw = keep.tile([P, H], U8, name="s1h_raw", align_bytes=64)
@@ -59,87 +69,91 @@ def tile_moe_hot_mlp_silu_kernel(
         gate_sb = keep.tile([P, TOP, T], F32, name="gate_sb")
         y = keep.tile([P, S], F32, name="y")
         ident = keep.tile([P, P], F32, name="ident")
-        warm = keep.tile([P, 8], F32, name="warm")
+        warm_in = keep.tile([P, 8], F32, name="warm_in")
         warm_out = keep.tile([P, 8], F32, name="warm_out")
 
-        nc.vector.memset(warm[:], 0.0)
-        nc.scalar.activation(warm_out[:], warm[:], SILU)
-        nc.vector.memset(s1c_first[:].bitcast(I32), 0)
-        nc.vector.memset(s1c_rest[:].bitcast(I32), 0)
-        nc.vector.memset(s2c[:].bitcast(I32), 0)
-        nc.vector.memset(s1h_raw[:].bitcast(I32), 0)
-        nc.vector.memset(s2h[:].bitcast(I32), 0)
+        def load_token_scales(q, queue):
+            queue.dma_start(
+                token_scales[32 * q : 32 * q + 32, :].bitcast(I32),
+                x_scales[0, 4 * q : 4 * q + 4, :].bitcast(I32).unsqueeze(0).broadcast_to([8, 4, T // 4]),
+            )
+
+        for q in range(QUADRANTS // 2, QUADRANTS):
+            load_token_scales(q, nc.scalar)
+
+        nc.vector.memset(warm_in[:], 0.0)
+        nc.scalar.activation(warm_out[:], warm_in[:], SILU)
+        for plane in (s1c_first, s1c_rest, s2c, s1h_raw, s2h):
+            nc.vector.memset(plane[:].bitcast(I32), 0)
         make_identity(nc, ident[:])
 
-        def load_scales(plane, scales, queue):
-            for q in range(4):
-                queue.dma_start(
+        def load_words(tile, words):
+            nc.sync.dma_start(tile[:].bitcast(I32), words.rearrange("e p b -> p e b").bitcast(I32))
+
+        def load_scales(plane, scales):
+            for q in range(QUADRANTS):
+                nc.sync.dma_start(
                     plane[32 * q : 32 * q + 4].bitcast(I32),
                     scales[:, 0, 4 * q : 4 * q + 4, :].rearrange("e b i -> b e i").bitcast(I32),
                 )
 
-        def load_scales_repeated(plane, rows):
-            words = rows.shape[1] // 4
-            for q in range(4):
-                nc.sync.dma_start(
-                    plane[32 * q : 32 * q + 32, :].bitcast(I32),
-                    rows[4 * q : 4 * q + 4, :].bitcast(I32).unsqueeze(0).broadcast_to([8, 4, words]),
-                )
-
-        load_scales_repeated(xs, x_scales[0])
+        for q in range(QUADRANTS // 2):
+            load_token_scales(q, nc.sync)
         nc.sync.dma_start(offs_sb[:], offs)
-        nc.sync.dma_start(xw[:], x_words[0].rearrange("p t d -> p (t d)").bitcast(I32))
-        nc.sync.dma_start(w1c_first[:].bitcast(I32), w1c_words[:2, 0].rearrange("f p b -> p f b").bitcast(I32))
-        load_scales(s1c_first, w1c_scales[:2], nc.sync)
+        nc.sync.dma_start(token_words[:], x_words[0].rearrange("p t d -> p (t d)").bitcast(I32))
+        load_words(w1c[0], w1c_words[0:2, 0])
+        load_scales(s1c_first, w1c_scales[:2])
+        load_words(w1c[1], w1c_words[2:4, 0])
+        load_words(w1c[2], w1c_words[4:6, 0])
         nc.sync.dma_start(w1h_raw[:], w1h_words[:, 0].rearrange("e p i d -> p e (i d)").bitcast(I32))
-        nc.sync.dma_start(w1c_mid[:].bitcast(I32), w1c_words[2:4, 0].rearrange("f p b -> p f b").bitcast(I32))
-        nc.sync.dma_start(w1c_last[:].bitcast(I32), w1c_words[4:, 0].rearrange("f p b -> p f b").bitcast(I32))
-        load_scales(s1c_rest, w1c_scales[2:], nc.sync)
-        for q in range(4):
+        load_scales(s1c_rest, w1c_scales[2:])
+        for q in range(QUADRANTS):
             nc.sync.dma_start(
                 s1h_raw[32 * q : 32 * q + 4 * HOT, :].bitcast(I32),
                 w1h_scales[:, 0, 4 * q : 4 * q + 4, :].bitcast(I32),
             )
-        nc.sync.dma_start(w2h[:].bitcast(I32), w2h_words[:, 0].rearrange("e p n d -> p e (n d)").bitcast(I32))
-        nc.sync.dma_start(w2c[:].bitcast(I32), w2c_words[:, 0].rearrange("f p b -> p f b").bitcast(I32))
-        load_scales(s2h, w2h_scales, nc.sync)
+        load_words(w2c, w2c_words[:, 0])
         nc.sync.dma_start(gate_sb[:], gate.rearrange("r p t -> p r t"))
+        load_scales(s2h, w2h_scales)
         for r, pos in enumerate((pos1, pos2, pos3)):
             nc.sync.dma_start(pos_sb[r][:], pos)
-        load_scales(s2c, w2c_scales, nc.sync)
+        load_scales(s2c, w2c_scales)
+        load_words(w2h, w2h_words[:, 0].rearrange("e p n d -> e p (n d)"))
 
-        def first_matrix(e):
-            f = e - HOT
-            words = (w1c_first, w1c_mid, w1c_last)[f // 2][:, f % 2, :]
-            scales = s1c_first[:, f, :] if f < 2 else s1c_rest[:, f - 2, :]
-            return words.bitcast(FP4X4), scales
+        slot_words, slot_scales = [], []
+        word_gathers, scale_gathers = list(WORD_GATHERS), list(SCALE_GATHERS)
 
-        def second_matrix(e):
-            if e < HOT:
-                return w2h[:, e, :].bitcast(FP8X4), s2h[:, e, :]
-            return w2c[:, e - HOT, :].bitcast(FP4X4), s2c[:, e - HOT, :]
+        def gather(done, blocks, window, dtype, name, tiles):
+            first_slot = ORDER[len(done) // BLOCKS] * C + len(done) % BLOCKS * P
+            tile = gathered.tile([P, blocks * P], dtype, name=name, bufs=tiles, align_bytes=64)
+            entries = offs_sb[:, first_slot // LIST_ROWS : (first_slot + blocks * P) // LIST_ROWS]
+            nc.vector.tensor_copy(tile[:], window.indirect(entries))
+            done.extend(tile[:, b * P : (b + 1) * P] for b in range(blocks))
 
-        def second_layer(group, step, first, width, w2, w2_scale, h_words, h_scales):
-            y_ps = psum_t.tile([P, width], F32, name="y_ps", tag=f"bank{(group + 1) % BANKS}")
-            nc.tensor.matmul_mx(
-                y_ps[:], lhsT=w2, lhsT_scale=w2_scale,
-                rhs=h_words[:].bitcast(FP8X4), rhs_scale=h_scales[:], start=True, stop=True,
+        def gather_up_to(blocks):
+            while min(len(slot_words), len(slot_scales)) < blocks:
+                if len(slot_scales) < len(slot_words):
+                    gather(slot_scales, scale_gathers.pop(0), token_scales[:], U8, "slot_scales", SCALE_TILES)
+                else:
+                    gather(slot_words, word_gathers.pop(0), token_words[:].bitcast(U32), U32, "slot_words", WORD_TILES)
+
+        def permute_columns(dst, src, run):
+            nc.vector.tensor_copy(
+                dst.rearrange("p (t c i) -> p c t i", t=PACK, i=run),
+                src.rearrange("p (c i t) -> p c t i", t=PACK, i=run),
             )
-            if group in Y_ON_VECTOR:
-                nc.vector.tensor_copy(y[:, first : first + width], y_ps[:])
-            else:
-                nc.scalar.copy(y[:, first : first + width], y_ps[:])
 
-        def hidden_cold(group, e, blocks, slot_words, slot_scales, grouped):
-            w1, w1_scale = first_matrix(e)
-            turned = psum_t.tile([P, len(blocks), 2, P], F32, name="turned", tag=f"bank{group % BANKS}")
-            hs = []
-            for b in blocks:
-                pre = psum_h.tile([P, H], F32, name="pre")
+        def hidden_cold(step, grouped):
+            w1 = w1c[step // 2][:, step % 2, :].bitcast(FP4X4)
+            w1_scale = s1c_first[:, step, :] if step < 2 else s1c_rest[:, step - 2, :]
+            turned = psum_shared.tile([P, BLOCKS, 2, P], F32, name="turned", tag=f"bank{step % SHARED_BANKS}")
+            halves = []
+            for b in range(BLOCKS):
+                pre = psum_first.tile([P, H], F32, name="pre")
                 nc.tensor.matmul_mx(
                     pre[:],
-                    lhsT=slot_words[:, b * P : (b + 1) * P].bitcast(FP8X4),
-                    lhsT_scale=slot_scales[:, b * P : (b + 1) * P],
+                    lhsT=slot_words[step * BLOCKS + b].bitcast(FP8X4),
+                    lhsT_scale=slot_scales[step * BLOCKS + b],
                     rhs=w1, rhs_scale=w1_scale, start=True, stop=True,
                 )
                 h = ring.tile([P, H], BF16, name="h")
@@ -148,107 +162,104 @@ def tile_moe_hot_mlp_silu_kernel(
                     pre[:].rearrange("s (p u d) -> s u p d", u=2, d=2),
                     SILU,
                 )
-                hs.append(h)
-            for j, h in enumerate(hs):
+                halves.append(h[:].bitcast(F32))
+            for b in range(BLOCKS):
                 for u in range(2):
-                    nc.tensor.transpose(
-                        turned[:, j, u, :], h[:].bitcast(F32)[:, u * P : (u + 1) * P], ident[:]
-                    )
-            (nc.vector.tensor_copy if group in TURN_ON_VECTOR else nc.scalar.copy)(
-                grouped[:].bitcast(F32).rearrange("p (b s u) -> p b s u", s=P, u=2),
+                    nc.tensor.transpose(turned[:, b, u, :], halves[b][:, u * P : (u + 1) * P], ident[:])
+            copy = nc.vector.tensor_copy if step in TURNED_ON_VECTOR else nc.scalar.copy
+            copy(
+                grouped.bitcast(F32).rearrange("p (b s u) -> p b s u", s=P, u=2),
                 turned[:].rearrange("p b u s -> p b s u"),
             )
 
-        def hidden_hot(e, blocks, slot_words, slot_scales, grouped, w1h, s1h):
-            for j, b in enumerate(blocks):
-                pre = psum_h.tile([P, H], F32, name="pre")
-                for t in range(4):
+        def hidden_hot(step, grouped, w1h, s1h):
+            e = step - COLD
+            for b in range(BLOCKS):
+                pre = psum_first.tile([P, H], F32, name="pre")
+                for t in range(PACK):
+                    cols = slice(t * P, (t + 1) * P)
                     nc.tensor.matmul_mx(
-                        pre[:, t * P : (t + 1) * P],
-                        lhsT=w1h[:, e, t * P : (t + 1) * P].bitcast(FP8X4),
-                        lhsT_scale=s1h[4 * e :, t * P : (t + 1) * P],
-                        rhs=slot_words[:, b * P : (b + 1) * P].bitcast(FP8X4),
-                        rhs_scale=slot_scales[:, b * P : (b + 1) * P],
+                        pre[:, cols],
+                        lhsT=w1h[:, e, cols].bitcast(FP8X4),
+                        lhsT_scale=s1h[4 * e :, cols],
+                        rhs=slot_words[step * BLOCKS + b].bitcast(FP8X4),
+                        rhs_scale=slot_scales[step * BLOCKS + b],
                         start=True, stop=True,
                     )
                 nc.scalar.activation(
-                    grouped[:, j * H : (j + 1) * H].rearrange("p (s t) -> p s t", t=4),
-                    pre[:].rearrange("p (t s) -> p s t", t=4),
+                    grouped[:, b * H : (b + 1) * H].rearrange("p (s t) -> p s t", t=PACK),
+                    pre[:].rearrange("p (t s) -> p s t", t=PACK),
                     SILU,
                 )
 
-        def permute_columns(dst, src, line):
-            nc.vector.tensor_copy(
-                dst.rearrange("p (t c i) -> p c t i", t=4, i=line),
-                src.rearrange("p (c i t) -> p c t i", t=4, i=line),
+        def second_layer(group, h_words, h_scales):
+            y_ps = psum_shared.tile(
+                [P, len(group) * C], F32, name="y_ps", tag=f"bank{(group[0] + 1) % SHARED_BANKS}"
             )
-
-        group = 0
-        waiting = None
-        for step, e in enumerate(ORDER):
-            if step == 4:
-                hot_first = keep.tile([P, HOT * 4 * H + H], U8, name="hot_first", align_bytes=64)
-                w1h = hot_first[:, : HOT * 4 * H].bitcast(I32).rearrange("p (e i) -> p e i", e=HOT)
-                s1h = hot_first[:, HOT * 4 * H :]
-                permute_columns(s1h, s1h_raw[:], 16)
-                for a in range(HOT):
-                    permute_columns(w1h[:, a, :], w1h_raw[:, a, :], 4)
-            slot_words = slots.tile([P, C], U32, name="slot_words", align_bytes=64)
-            slot_scales = slots.tile([P, C], U8, name="slot_scales", align_bytes=64, bufs=2)
-            col = e * C // 16
-            pieces = 2 if step in (0, 8, ) else 1
-            for a in range(pieces):
-                w = C // pieces
-                piece = offs_sb[:, col + a * w // 16 : col + (a + 1) * w // 16]
-                nc.vector.tensor_copy(slot_scales[:, a * w : (a + 1) * w], xs[:].indirect(piece))
-                nc.vector.tensor_copy(slot_words[:, a * w : (a + 1) * w], xw[:].bitcast(U32).indirect(piece))
-
-            w2, w2_scale = second_matrix(e)
-            groups = [[0], [1]] if step in () else [[0, 1]]
-            for blocks in groups:
-                width = P * len(blocks)
-                grouped = ring.tile([P, 4 * width], BF16, name="grouped", align_bytes=64)
-                if e < HOT:
-                    hidden_hot(e, blocks, slot_words, slot_scales, grouped, w1h, s1h)
+            for place, step in enumerate(group):
+                if step < COLD:
+                    w2, w2_scale = w2c[:, step, :].bitcast(FP4X4), s2c[:, step, :]
                 else:
-                    hidden_cold(group, e, blocks, slot_words, slot_scales, grouped)
-                h_words = ring.tile([P, width], U32, name="h_words", align_bytes=64)
-                h_scales = ring.tile([P, width], U8, name="h_scales", align_bytes=64)
-                nc.vector.quantize_mx(h_words[:].bitcast(FP8X4), h_scales[:], grouped[:])
-                if waiting is not None:
-                    second_layer(*waiting)
-                waiting = (group, step, e * C + blocks[0] * P, width, w2, w2_scale, h_words, h_scales)
-                group += 1
-        second_layer(*waiting)
+                    w2, w2_scale = w2h[:, step - COLD, :].bitcast(FP8X4), s2h[:, step - COLD, :]
+                cols = slice(place * C, (place + 1) * C)
+                nc.tensor.matmul_mx(
+                    y_ps[:, cols], lhsT=w2, lhsT_scale=w2_scale,
+                    rhs=h_words[:, cols].bitcast(FP8X4), rhs_scale=h_scales[:, cols], start=True, stop=True,
+                )
+            first_slot = ORDER[group[0]] * C
+            copy = nc.vector.tensor_copy if group[-1] in RESULT_ON_VECTOR else nc.scalar.copy
+            copy(y[:, first_slot : first_slot + len(group) * C], y_ps[:])
+
+        for group in GROUPS:
+            grouped = ring.tile([P, len(group), PACK * C], BF16, name="grouped", align_bytes=64)
+            for place, step in enumerate(group):
+                if step == COLD:
+                    hot = keep.tile([P, HOT * PACK * H + H], U8, name="hot", tag="w1c1", align_bytes=64)
+                    w1h = hot[:, : HOT * PACK * H].bitcast(I32).rearrange("p (e i) -> p e i", e=HOT)
+                    s1h = hot[:, HOT * PACK * H :]
+                    permute_columns(s1h, s1h_raw[:], 16)
+                    for e in range(HOT):
+                        permute_columns(w1h[:, e, :], w1h_raw[:, e, :], 4)
+                gather_up_to((step + 1) * BLOCKS)
+                if step < COLD:
+                    hidden_cold(step, grouped[:, place, :])
+                else:
+                    hidden_hot(step, grouped[:, place, :], w1h, s1h)
+            h_words = ring.tile([P, len(group) * C], U32, name="h_words", align_bytes=64)
+            h_scales = ring.tile([P, len(group) * C], U8, name="h_scales", align_bytes=64)
+            nc.vector.quantize_mx(
+                h_words[:].bitcast(FP8X4), h_scales[:], grouped[:].rearrange("p g x -> p (g x)")
+            )
+            second_layer(group, h_words, h_scales)
 
         for chunk, (lo, hi) in enumerate(TOKEN_CHUNKS):
             width = hi - lo
             parts = []
             for r in range(TOP):
-                part = keep.tile([P, width], F32, name=f"part{r}_{lo}")
-                nc.vector.tensor_tensor(
-                    part[:], y[:].indirect(pos_sb[r][:, lo // 16 : hi // 16]), gate_sb[:, r, lo:hi], MULT
-                )
+                part = keep.tile([P, width], F32, name=f"part{r}_{chunk}")
+                entries = pos_sb[r][:, lo // LIST_ROWS : hi // LIST_ROWS]
+                nc.vector.tensor_tensor(part[:], y[:].indirect(entries), gate_sb[:, r, lo:hi], MULT)
                 parts.append(part)
-            total = keep.tile([P, width], F32, name=f"total{lo}")
+            total = keep.tile([P, width], F32, name=f"total{chunk}")
             if chunk < SUMMED_IN_PSUM:
-                sum_sb = keep.tile([P, width], F32, name=f"sum_sb{lo}")
+                sum_sb = keep.tile([P, width], F32, name=f"sum_sb{chunk}")
                 for b in range(width // P):
                     cols = slice(b * P, (b + 1) * P)
-                    sum_ps = psum_t.tile([P, P], F32, name="sum_ps", tag=f"bank{(lo // P + b + 1) % BANKS}")
+                    sum_ps = psum_shared.tile([P, P], F32, name="sum_ps", tag=f"bank{lo // P + b}")
                     for r in range(TOP):
                         nc.tensor.matmul(
                             sum_ps[:], parts[r][:, cols], ident[:],
                             start=(r == 0), stop=(r == TOP - 1), is_transpose=True,
                         )
                     nc.scalar.copy(sum_sb[:, cols], sum_ps[:])
-                back_ps = psum_h.tile([P, width], F32, name="pre")
+                back_ps = psum_first.tile([P, width], F32, name="back_ps", tag="pre")
                 for b in range(width // P):
                     cols = slice(b * P, (b + 1) * P)
                     nc.tensor.transpose(back_ps[:, cols], sum_sb[:, cols], ident[:])
                 nc.scalar.copy(total[:], back_ps[:])
+                nc.scalar.dma_start(out[:, lo:hi], total[:])
             else:
-                pair = keep.tile([P, width], F32, name=f"pair{lo}")
+                pair = keep.tile([P, width], F32, name=f"pair{chunk}")
                 nc.vector.tensor_tensor(pair[:], parts[0][:], parts[1][:], ADD)
                 nc.vector.tensor_tensor(total[:], pair[:], parts[2][:], ADD)
-            (nc.scalar if chunk < SUMMED_IN_PSUM else nc.sync).dma_start(out[:, lo:hi], total[:])
+                nc.sync.dma_start(out[:, lo:hi], total[:])

@@ -27,10 +27,10 @@ MULT = mybir.AluOpType.mult
 ADD = mybir.AluOpType.add
 
 ORDER = list(range(HOT, E)) + list(range(HOT))
-WORD_GATHERS = [1, 2, 3, 2, 2, 2, 2, 4]
-SCALE_GATHERS = [2, 2, 1, 3, 4, 4, 2]
-WORD_TILES, SCALE_TILES = 4, 3
-TURNED_ON_VECTOR = (5,)
+WORD_GATHERS = [1, 1, 4, 1, 4, 1, 4, 2]
+SCALE_GATHERS = [2, 1, 1, 3, 2, 3, 3, 3]
+WORD_TILES, SCALE_TILES = 3, 3
+TURNED_ON_VECTOR = (2, 5,)
 RESULT_ON_VECTOR = (1, 7,)
 GROUPS = [(0, 1), (2, 3), (4, 5), (6, 7), (8,)]
 FIRST_BANKS = 3
@@ -46,7 +46,7 @@ def tile_moe_hot_mlp_silu_kernel(
     nc = tc.nc
     with ExitStack() as ctx:
         keep = ctx.enter_context(tc.tile_pool(name="keep", bufs=1))
-        ring = ctx.enter_context(tc.tile_pool(name="ring", bufs=5))
+        ring = ctx.enter_context(tc.tile_pool(name="ring", bufs=7))
         gathered = ctx.enter_context(tc.tile_pool(name="gathered", bufs=WORD_TILES))
         psum_first = ctx.enter_context(tc.psum_pool(name="psum_first", bufs=FIRST_BANKS))
         psum_shared = ctx.enter_context(tc.psum_pool(name="psum_shared", bufs=1))
@@ -103,22 +103,22 @@ def tile_moe_hot_mlp_silu_kernel(
         nc.sync.dma_start(token_words[:], x_words[0].rearrange("p t d -> p (t d)").bitcast(I32))
         load_words(w1c[0], w1c_words[0:2, 0])
         load_scales(s1c_first, w1c_scales[:2])
+        load_words(w2c, w2c_words[:, 0])
         load_words(w1c[1], w1c_words[2:4, 0])
         load_words(w1c[2], w1c_words[4:6, 0])
-        nc.sync.dma_start(w1h_raw[:], w1h_words[:, 0].rearrange("e p i d -> p e (i d)").bitcast(I32))
         load_scales(s1c_rest, w1c_scales[2:])
         for q in range(QUADRANTS):
             nc.sync.dma_start(
                 s1h_raw[32 * q : 32 * q + 4 * HOT, :].bitcast(I32),
                 w1h_scales[:, 0, 4 * q : 4 * q + 4, :].bitcast(I32),
             )
-        load_words(w2c, w2c_words[:, 0])
+        nc.sync.dma_start(w1h_raw[:], w1h_words[:, 0].rearrange("e p i d -> p e (i d)").bitcast(I32))
         nc.sync.dma_start(gate_sb[:], gate.rearrange("r p t -> p r t"))
-        load_scales(s2h, w2h_scales)
         for r, pos in enumerate((pos1, pos2, pos3)):
             nc.sync.dma_start(pos_sb[r][:], pos)
-        load_scales(s2c, w2c_scales)
         load_words(w2h, w2h_words[:, 0].rearrange("e p n d -> e p (n d)"))
+        load_scales(s2c, w2c_scales)
+        load_scales(s2h, w2h_scales)
 
         slot_words, slot_scales = [], []
         word_gathers, scale_gathers = list(WORD_GATHERS), list(SCALE_GATHERS)
@@ -138,7 +138,7 @@ def tile_moe_hot_mlp_silu_kernel(
                     gather(slot_words, word_gathers.pop(0), token_words[:].bitcast(U32), U32, "slot_words", WORD_TILES)
 
         def permute_columns(dst, src, run):
-            nc.vector.tensor_copy(
+            nc.gpsimd.tensor_copy(
                 dst.rearrange("p (t c i) -> p c t i", t=PACK, i=run),
                 src.rearrange("p (c i t) -> p c t i", t=PACK, i=run),
             )

@@ -27,15 +27,15 @@ MULT = mybir.AluOpType.mult
 ADD = mybir.AluOpType.add
 
 ORDER = list(range(HOT, E)) + list(range(HOT))
-WORD_GATHERS = [1, 1, 4, 1, 4, 1, 4, 2]
-SCALE_GATHERS = [2, 1, 1, 3, 2, 3, 3, 3]
-WORD_TILES, SCALE_TILES = 3, 3
-TURNED_ON_VECTOR = (2, 5,)
-RESULT_ON_VECTOR = (1, 7,)
+WORD_GATHERS = [1, 1, 2, 4, 4, 4, 2]
+SCALE_GATHERS = [1, 1, 2, 4, 4, 4, 2]
+TURNED_ON_VECTOR = (4, 5)
+RESULT_ON_VECTOR = (7, 8)
+RESULT_BANK = {1: 0, 3: 1, 5: 2, 7: 3, 8: 7}
 GROUPS = [(0, 1), (2, 3), (4, 5), (6, 7), (8,)]
 FIRST_BANKS = 3
 SHARED_BANKS = 5
-TOKEN_CHUNKS = [(0, 384), (384, 512), (512, 640), (640, 768)]
+TOKEN_CHUNKS = [(0, 384), (384, 512), (512, 768)]
 SUMMED_IN_PSUM = 2
 
 
@@ -47,8 +47,6 @@ def tile_moe_hot_mlp_silu_kernel(
     with ExitStack() as ctx:
         keep = ctx.enter_context(tc.tile_pool(name="keep", bufs=1))
         ring = ctx.enter_context(tc.tile_pool(name="ring", bufs=7))
-        gathered = ctx.enter_context(tc.tile_pool(name="gathered", bufs=WORD_TILES))
-        psum_first = ctx.enter_context(tc.psum_pool(name="psum_first", bufs=FIRST_BANKS))
         psum_shared = ctx.enter_context(tc.psum_pool(name="psum_shared", bufs=1))
 
         offs_sb = keep.tile([P, S // LIST_ROWS], U16, name="offs_sb")
@@ -63,7 +61,7 @@ def tile_moe_hot_mlp_silu_kernel(
         w2h = keep.tile([P, HOT, PACK * N], U8, name="w2h", align_bytes=64)
         s1c_first = keep.tile([P, 2, H], U8, name="s1c_first", align_bytes=64)
         s1c_rest = keep.tile([P, COLD - 2, H], U8, name="s1c_rest", align_bytes=64)
-        s1h_raw = keep.tile([P, H], U8, name="s1h_raw", align_bytes=64)
+        s1h_raw = keep.tile([P, HOT, H], U8, name="s1h_raw", align_bytes=64)
         s2c = keep.tile([P, COLD, N], U8, name="s2c", align_bytes=64)
         s2h = keep.tile([P, HOT, N], U8, name="s2h", align_bytes=64)
         gate_sb = keep.tile([P, TOP, T], F32, name="gate_sb")
@@ -78,11 +76,7 @@ def tile_moe_hot_mlp_silu_kernel(
                 x_scales[0, 4 * q : 4 * q + 4, :].bitcast(I32).unsqueeze(0).broadcast_to([8, 4, T // 4]),
             )
 
-        for q in range(QUADRANTS // 2, QUADRANTS):
-            load_token_scales(q, nc.scalar)
-
         nc.vector.memset(warm_in[:], 0.0)
-        nc.scalar.activation(warm_out[:], warm_in[:], SILU)
         for plane in (s1c_first, s1c_rest, s2c, s1h_raw, s2h):
             nc.vector.memset(plane[:].bitcast(I32), 0)
         make_identity(nc, ident[:])
@@ -97,45 +91,40 @@ def tile_moe_hot_mlp_silu_kernel(
                     scales[:, 0, 4 * q : 4 * q + 4, :].rearrange("e b i -> b e i").bitcast(I32),
                 )
 
-        for q in range(QUADRANTS // 2):
-            load_token_scales(q, nc.sync)
+        for q in range(QUADRANTS):
+            load_token_scales(q, nc.sync if q < QUADRANTS // 2 else nc.scalar)
         nc.sync.dma_start(offs_sb[:], offs)
         nc.sync.dma_start(token_words[:], x_words[0].rearrange("p t d -> p (t d)").bitcast(I32))
+        nc.scalar.activation(warm_out[:], warm_in[:], SILU)
         load_words(w1c[0], w1c_words[0:2, 0])
         load_scales(s1c_first, w1c_scales[:2])
-        load_words(w2c, w2c_words[:, 0])
         load_words(w1c[1], w1c_words[2:4, 0])
-        load_words(w1c[2], w1c_words[4:6, 0])
         load_scales(s1c_rest, w1c_scales[2:])
-        for q in range(QUADRANTS):
-            nc.sync.dma_start(
-                s1h_raw[32 * q : 32 * q + 4 * HOT, :].bitcast(I32),
-                w1h_scales[:, 0, 4 * q : 4 * q + 4, :].bitcast(I32),
-            )
+        load_words(w1c[2], w1c_words[4:6, 0])
+        load_scales(s1h_raw, w1h_scales)
         nc.sync.dma_start(w1h_raw[:], w1h_words[:, 0].rearrange("e p i d -> p e (i d)").bitcast(I32))
-        nc.sync.dma_start(gate_sb[:], gate.rearrange("r p t -> p r t"))
+        load_words(w2c, w2c_words[:, 0])
+        load_scales(s2c, w2c_scales)
+        load_words(w2h, w2h_words[:, 0].rearrange("e p n d -> e p (n d)"))
+        load_scales(s2h, w2h_scales)
         for r, pos in enumerate((pos1, pos2, pos3)):
             nc.sync.dma_start(pos_sb[r][:], pos)
-        load_words(w2h, w2h_words[:, 0].rearrange("e p n d -> e p (n d)"))
-        load_scales(s2c, w2c_scales)
-        load_scales(s2h, w2h_scales)
+        nc.sync.dma_start(gate_sb[:], gate.rearrange("r p t -> p r t"))
 
         slot_words, slot_scales = [], []
-        word_gathers, scale_gathers = list(WORD_GATHERS), list(SCALE_GATHERS)
 
-        def gather(done, blocks, window, dtype, name, tiles):
+        def gather(done, blocks, window, dtype, tag):
             first_slot = ORDER[len(done) // BLOCKS] * C + len(done) % BLOCKS * P
-            tile = gathered.tile([P, blocks * P], dtype, name=name, bufs=tiles, align_bytes=64)
+            tile = keep.tile([P, blocks * P], dtype, name=tag, tag=tag, align_bytes=64)
             entries = offs_sb[:, first_slot // LIST_ROWS : (first_slot + blocks * P) // LIST_ROWS]
             nc.vector.tensor_copy(tile[:], window.indirect(entries))
             done.extend(tile[:, b * P : (b + 1) * P] for b in range(blocks))
 
-        def gather_up_to(blocks):
-            while min(len(slot_words), len(slot_scales)) < blocks:
-                if len(slot_scales) < len(slot_words):
-                    gather(slot_scales, scale_gathers.pop(0), token_scales[:], U8, "slot_scales", SCALE_TILES)
-                else:
-                    gather(slot_words, word_gathers.pop(0), token_words[:].bitcast(U32), U32, "slot_words", WORD_TILES)
+        def gather_scales(blocks, place):
+            gather(slot_scales, blocks, token_scales[:], U8, f"slot_scales{place}")
+
+        def gather_words(blocks, place):
+            gather(slot_words, blocks, token_words[:].bitcast(U32), U32, f"slot_words{place}")
 
         def permute_columns(dst, src, run):
             nc.gpsimd.tensor_copy(
@@ -143,13 +132,12 @@ def tile_moe_hot_mlp_silu_kernel(
                 src.rearrange("p (c i t) -> p c t i", t=PACK, i=run),
             )
 
-        def hidden_cold(step, grouped):
+        def hidden_cold(step):
             w1 = w1c[step // 2][:, step % 2, :].bitcast(FP4X4)
             w1_scale = s1c_first[:, step, :] if step < 2 else s1c_rest[:, step - 2, :]
-            turned = psum_shared.tile([P, BLOCKS, 2, P], F32, name="turned", tag=f"bank{step % SHARED_BANKS}")
             halves = []
             for b in range(BLOCKS):
-                pre = psum_first.tile([P, H], F32, name="pre")
+                pre = psum_shared.tile([P, H], F32, name="pre", tag=f"bank{(step * BLOCKS + b) % 3}")
                 nc.tensor.matmul_mx(
                     pre[:],
                     lhsT=slot_words[step * BLOCKS + b].bitcast(FP8X4),
@@ -163,6 +151,10 @@ def tile_moe_hot_mlp_silu_kernel(
                     SILU,
                 )
                 halves.append(h[:].bitcast(F32))
+            return halves
+
+        def turn_cold(step, halves, grouped):
+            turned = psum_shared.tile([P, BLOCKS, 2, P], F32, name="turned", tag="bank3" if step < COLD - 1 else "bank7")
             for b in range(BLOCKS):
                 for u in range(2):
                     nc.tensor.transpose(turned[:, b, u, :], halves[b][:, u * P : (u + 1) * P], ident[:])
@@ -175,13 +167,13 @@ def tile_moe_hot_mlp_silu_kernel(
         def hidden_hot(step, grouped, w1h, s1h):
             e = step - COLD
             for b in range(BLOCKS):
-                pre = psum_first.tile([P, H], F32, name="pre")
+                pre = psum_shared.tile([P, H], F32, name="pre", tag=f"bank{(step * BLOCKS + b) % 3 + (4 if step * BLOCKS + b >= 15 else 0)}")
                 for t in range(PACK):
                     cols = slice(t * P, (t + 1) * P)
                     nc.tensor.matmul_mx(
                         pre[:, cols],
                         lhsT=w1h[:, e, cols].bitcast(FP8X4),
-                        lhsT_scale=s1h[4 * e :, cols],
+                        lhsT_scale=s1h[:, e, cols],
                         rhs=slot_words[step * BLOCKS + b].bitcast(FP8X4),
                         rhs_scale=slot_scales[step * BLOCKS + b],
                         start=True, stop=True,
@@ -194,7 +186,7 @@ def tile_moe_hot_mlp_silu_kernel(
 
         def second_layer(group, h_words, h_scales):
             y_ps = psum_shared.tile(
-                [P, len(group) * C], F32, name="y_ps", tag=f"bank{(group[0] + 1) % SHARED_BANKS}"
+                [P, len(group) * C], F32, name="y_ps", tag=f"bank{RESULT_BANK[group[-1]]}"
             )
             for place, step in enumerate(group):
                 if step < COLD:
@@ -210,21 +202,34 @@ def tile_moe_hot_mlp_silu_kernel(
             copy = nc.vector.tensor_copy if group[-1] in RESULT_ON_VECTOR else nc.scalar.copy
             copy(y[:, first_slot : first_slot + len(group) * C], y_ps[:])
 
-        for group in GROUPS:
-            grouped = ring.tile([P, len(group), PACK * C], BF16, name="grouped", align_bytes=64)
-            for place, step in enumerate(group):
-                if step == COLD:
-                    hot = keep.tile([P, HOT * PACK * H + H], U8, name="hot", tag="w1c1", align_bytes=64)
-                    w1h = hot[:, : HOT * PACK * H].bitcast(I32).rearrange("p (e i) -> p e i", e=HOT)
-                    s1h = hot[:, HOT * PACK * H :]
-                    permute_columns(s1h, s1h_raw[:], 16)
-                    for e in range(HOT):
-                        permute_columns(w1h[:, e, :], w1h_raw[:, e, :], 4)
-                gather_up_to((step + 1) * BLOCKS)
-                if step < COLD:
-                    hidden_cold(step, grouped[:, place, :])
-                else:
-                    hidden_hot(step, grouped[:, place, :], w1h, s1h)
+        for b in range(4):
+            gather_scales(1, b)
+        for b in range(4):
+            gather_words(1, b)
+        gather_words(4, 4)
+        w1h = keep.tile([P, HOT, H], I32, name="w1h", align_bytes=64)
+        s1h = keep.tile([P, HOT, H], U8, name="s1h", align_bytes=64)
+        for e in range(HOT):
+            permute_columns(s1h[:, e, :], s1h_raw[:, e, :], 16)
+            permute_columns(w1h[:, e, :], w1h_raw[:, e, :], 4)
+        hidden = [
+            keep.tile([P, len(group), PACK * C], BF16, name=f"grouped{group[0]}", align_bytes=64) for group in GROUPS
+        ]
+        halves = None
+        for step in range(E):
+            waiting = halves
+            if step == 2:
+                for b, (scale_blocks, word_blocks) in enumerate([(4, 4), (4, 4), (4, 2)]):
+                    gather_scales(scale_blocks, b)
+                    gather_words(word_blocks, b)
+                gather_scales(2, 3)
+            if step < COLD:
+                halves = hidden_cold(step)
+            else:
+                hidden_hot(step, hidden[step // 2][:, step % 2, :], w1h, s1h)
+            if 0 < step <= COLD:
+                turn_cold(step - 1, waiting, hidden[(step - 1) // 2][:, (step - 1) % 2, :])
+        for group, grouped in zip(GROUPS, hidden):
             h_words = ring.tile([P, len(group) * C], U32, name="h_words", align_bytes=64)
             h_scales = ring.tile([P, len(group) * C], U8, name="h_scales", align_bytes=64)
             nc.vector.quantize_mx(
@@ -252,7 +257,7 @@ def tile_moe_hot_mlp_silu_kernel(
                             start=(r == 0), stop=(r == TOP - 1), is_transpose=True,
                         )
                     nc.scalar.copy(sum_sb[:, cols], sum_ps[:])
-                back_ps = psum_first.tile([P, width], F32, name="back_ps", tag="pre")
+                back_ps = psum_shared.tile([P, width], F32, name="back_ps", tag=f"bank{5 + chunk}")
                 for b in range(width // P):
                     cols = slice(b * P, (b + 1) * P)
                     nc.tensor.transpose(back_ps[:, cols], sum_sb[:, cols], ident[:])

@@ -29,9 +29,9 @@ ADD = mybir.AluOpType.add
 ORDER = list(range(HOT, E)) + list(range(HOT))
 WORD_GATHERS = [1, 1, 2, 4, 4, 4, 2]
 SCALE_GATHERS = [1, 1, 2, 4, 4, 4, 2]
-TURNED_ON_VECTOR = (4, 5)
-RESULT_ON_VECTOR = (7, 8)
-RESULT_BANK = {1: 0, 3: 1, 5: 2, 7: 3, 8: 7}
+TURNED_ON_VECTOR = (3, 4, 5)
+RESULT_ON_VECTOR = (1, 7, 8)
+RESULT_BANK = {1: 1, 3: 2, 5: 0, 7: 3, 8: 7}
 GROUPS = [(0, 1), (2, 3), (4, 5), (6, 7), (8,)]
 FIRST_BANKS = 3
 SHARED_BANKS = 5
@@ -154,7 +154,7 @@ def tile_moe_hot_mlp_silu_kernel(
             return halves
 
         def turn_cold(step, halves, grouped):
-            turned = psum_shared.tile([P, BLOCKS, 2, P], F32, name="turned", tag="bank3" if step < COLD - 1 else "bank7")
+            turned = psum_shared.tile([P, BLOCKS, 2, P], F32, name="turned", tag=f"bank{ {4: 7, 5: 6}.get(step, 3)}")
             for b in range(BLOCKS):
                 for u in range(2):
                     nc.tensor.transpose(turned[:, b, u, :], halves[b][:, u * P : (u + 1) * P], ident[:])
@@ -167,7 +167,7 @@ def tile_moe_hot_mlp_silu_kernel(
         def hidden_hot(step, grouped, w1h, s1h):
             e = step - COLD
             for b in range(BLOCKS):
-                pre = psum_shared.tile([P, H], F32, name="pre", tag=f"bank{(step * BLOCKS + b) % 3 + (4 if step * BLOCKS + b >= 15 else 0)}")
+                pre = psum_shared.tile([P, H], F32, name="pre", tag=f"bank{(step * BLOCKS + b) % 3 if step < E - 1 else 4 + b}")
                 for t in range(PACK):
                     cols = slice(t * P, (t + 1) * P)
                     nc.tensor.matmul_mx(

@@ -11,6 +11,8 @@ FLOPS = 2 * S * (K * H + H * N)
 P = 128
 PACK = 4
 QUADRANTS = 4
+QUADRANT = P // QUADRANTS
+QUADRANT_ROWS = 4
 LIST_ROWS = 16
 BLOCKS = C // P
 
@@ -27,16 +29,16 @@ MULT = mybir.AluOpType.mult
 ADD = mybir.AluOpType.add
 
 ORDER = list(range(HOT, E)) + list(range(HOT))
-WORD_GATHERS = [1, 1, 2, 4, 4, 4, 2]
-SCALE_GATHERS = [1, 1, 2, 4, 4, 4, 2]
-TURNED_ON_VECTOR = (3, 4, 5)
-RESULT_ON_VECTOR = (1, 7, 8)
-RESULT_BANK = {1: 1, 3: 2, 5: 0, 7: 3, 8: 7}
 GROUPS = [(0, 1), (2, 3), (4, 5), (6, 7), (8,)]
-FIRST_BANKS = 3
-SHARED_BANKS = 5
-TOKEN_CHUNKS = [(0, 384), (384, 512), (512, 768)]
+TURNED_ON_SCALAR = 3
+RESULTS_ON_SCALAR = 3
+RING = 3
+LAST_EXPERT_BANKS = (4, 5)
+TURN_BANKS = (3, 3, 3, 3, 7, 6)
+RESULT_BANKS = (1, 2, 0, 3, 7)
+TOKEN_CHUNKS = [(0, 384), (384, 512), (512, 640), (640, 768)]
 SUMMED_IN_PSUM = 2
+BACK_BANKS = (5, 6)
 
 
 def tile_moe_hot_mlp_silu_kernel(
@@ -47,15 +49,13 @@ def tile_moe_hot_mlp_silu_kernel(
     with ExitStack() as ctx:
         keep = ctx.enter_context(tc.tile_pool(name="keep", bufs=1))
         ring = ctx.enter_context(tc.tile_pool(name="ring", bufs=7))
-        psum_shared = ctx.enter_context(tc.psum_pool(name="psum_shared", bufs=1))
+        psum = ctx.enter_context(tc.psum_pool(name="psum", bufs=1))
 
         offs_sb = keep.tile([P, S // LIST_ROWS], U16, name="offs_sb")
         pos_sb = [keep.tile([P, T // LIST_ROWS], U16, name=f"pos_sb{r}") for r in range(TOP)]
         token_words = keep.tile([P, T], I32, name="token_words", align_bytes=64)
         token_scales = keep.tile([P, T], U8, name="token_scales", align_bytes=64)
-        w1c = [
-            keep.tile([P, 2, 2 * H], U8, name=f"w1c{a}", tag=f"w1c{a}", align_bytes=64) for a in range(COLD // 2)
-        ]
+        w1c = [keep.tile([P, 2, 2 * H], U8, name=f"w1c{a}", align_bytes=64) for a in range(COLD // 2)]
         w1h_raw = keep.tile([P, HOT, H], I32, name="w1h_raw", align_bytes=64)
         w2c = keep.tile([P, COLD, 2 * N], U8, name="w2c", align_bytes=64)
         w2h = keep.tile([P, HOT, PACK * N], U8, name="w2h", align_bytes=64)
@@ -70,12 +70,6 @@ def tile_moe_hot_mlp_silu_kernel(
         warm_in = keep.tile([P, 8], F32, name="warm_in")
         warm_out = keep.tile([P, 8], F32, name="warm_out")
 
-        def load_token_scales(q, queue):
-            queue.dma_start(
-                token_scales[32 * q : 32 * q + 32, :].bitcast(I32),
-                x_scales[0, 4 * q : 4 * q + 4, :].bitcast(I32).unsqueeze(0).broadcast_to([8, 4, T // 4]),
-            )
-
         nc.vector.memset(warm_in[:], 0.0)
         for plane in (s1c_first, s1c_rest, s2c, s1h_raw, s2h):
             nc.vector.memset(plane[:].bitcast(I32), 0)
@@ -85,14 +79,19 @@ def tile_moe_hot_mlp_silu_kernel(
             nc.sync.dma_start(tile[:].bitcast(I32), words.rearrange("e p b -> p e b").bitcast(I32))
 
         def load_scales(plane, scales):
-            for q in range(QUADRANTS):
+            for j in range(QUADRANT_ROWS):
                 nc.sync.dma_start(
-                    plane[32 * q : 32 * q + 4].bitcast(I32),
-                    scales[:, 0, 4 * q : 4 * q + 4, :].rearrange("e b i -> b e i").bitcast(I32),
+                    plane[j:P:QUADRANT].bitcast(I32),
+                    scales[:, 0, j::QUADRANT_ROWS, :].rearrange("e q i -> q e i").bitcast(I32),
                 )
 
         for q in range(QUADRANTS):
-            load_token_scales(q, nc.sync if q < QUADRANTS // 2 else nc.scalar)
+            queue = nc.sync if q < QUADRANTS // 2 else nc.scalar
+            rows = x_scales[0, QUADRANT_ROWS * q : QUADRANT_ROWS * (q + 1), :].bitcast(I32)
+            queue.dma_start(
+                token_scales[QUADRANT * q : QUADRANT * (q + 1), :].bitcast(I32),
+                rows.unsqueeze(0).broadcast_to([QUADRANT // QUADRANT_ROWS, QUADRANT_ROWS, T // 4]),
+            )
         nc.sync.dma_start(offs_sb[:], offs)
         nc.sync.dma_start(token_words[:], x_words[0].rearrange("p t d -> p (t d)").bitcast(I32))
         nc.scalar.activation(warm_out[:], warm_in[:], SILU)
@@ -100,9 +99,9 @@ def tile_moe_hot_mlp_silu_kernel(
         load_scales(s1c_first, w1c_scales[:2])
         load_words(w1c[1], w1c_words[2:4, 0])
         load_scales(s1c_rest, w1c_scales[2:])
+        nc.sync.dma_start(w1h_raw[:], w1h_words[:, 0].rearrange("e p i d -> p e (i d)").bitcast(I32))
         load_words(w1c[2], w1c_words[4:6, 0])
         load_scales(s1h_raw, w1h_scales)
-        nc.sync.dma_start(w1h_raw[:], w1h_words[:, 0].rearrange("e p i d -> p e (i d)").bitcast(I32))
         load_words(w2c, w2c_words[:, 0])
         load_scales(s2c, w2c_scales)
         load_words(w2h, w2h_words[:, 0].rearrange("e p n d -> e p (n d)"))
@@ -111,20 +110,14 @@ def tile_moe_hot_mlp_silu_kernel(
             nc.sync.dma_start(pos_sb[r][:], pos)
         nc.sync.dma_start(gate_sb[:], gate.rearrange("r p t -> p r t"))
 
-        slot_words, slot_scales = [], []
+        def gather(tile, tile_first, first, blocks, window):
+            slot = ORDER[first // BLOCKS] * C + first % BLOCKS * P
+            entries = offs_sb[:, slot // LIST_ROWS : (slot + blocks * P) // LIST_ROWS]
+            column = (first - tile_first) * P
+            nc.vector.tensor_copy(tile[:, column : column + blocks * P], window.indirect(entries))
 
-        def gather(done, blocks, window, dtype, tag):
-            first_slot = ORDER[len(done) // BLOCKS] * C + len(done) % BLOCKS * P
-            tile = keep.tile([P, blocks * P], dtype, name=tag, tag=tag, align_bytes=64)
-            entries = offs_sb[:, first_slot // LIST_ROWS : (first_slot + blocks * P) // LIST_ROWS]
-            nc.vector.tensor_copy(tile[:], window.indirect(entries))
-            done.extend(tile[:, b * P : (b + 1) * P] for b in range(blocks))
-
-        def gather_scales(blocks, place):
-            gather(slot_scales, blocks, token_scales[:], U8, f"slot_scales{place}")
-
-        def gather_words(blocks, place):
-            gather(slot_words, blocks, token_words[:].bitcast(U32), U32, f"slot_words{place}")
+        def block_slices(tile):
+            return [tile[:, column : column + P] for column in range(0, tile.shape[1], P)]
 
         def permute_columns(dst, src, run):
             nc.gpsimd.tensor_copy(
@@ -132,12 +125,15 @@ def tile_moe_hot_mlp_silu_kernel(
                 src.rearrange("p (c i t) -> p c t i", t=PACK, i=run),
             )
 
-        def hidden_cold(step):
+        def first_bank(step, b):
+            return f"bank{(step * BLOCKS + b) % RING if step < E - 1 else LAST_EXPERT_BANKS[b]}"
+
+        def hidden_cold(step, blocks):
             w1 = w1c[step // 2][:, step % 2, :].bitcast(FP4X4)
             w1_scale = s1c_first[:, step, :] if step < 2 else s1c_rest[:, step - 2, :]
-            halves = []
-            for b in range(BLOCKS):
-                pre = psum_shared.tile([P, H], F32, name="pre", tag=f"bank{(step * BLOCKS + b) % 3}")
+            pairs = []
+            for b in blocks:
+                pre = psum.tile([P, H], F32, name="pre", tag=first_bank(step, b))
                 nc.tensor.matmul_mx(
                     pre[:],
                     lhsT=slot_words[step * BLOCKS + b].bitcast(FP8X4),
@@ -150,24 +146,24 @@ def tile_moe_hot_mlp_silu_kernel(
                     pre[:].rearrange("s (p u d) -> s u p d", u=2, d=2),
                     SILU,
                 )
-                halves.append(h[:].bitcast(F32))
-            return halves
+                pairs.append(h[:].bitcast(F32))
+            return pairs
 
-        def turn_cold(step, halves, grouped):
-            turned = psum_shared.tile([P, BLOCKS, 2, P], F32, name="turned", tag=f"bank{ {4: 7, 5: 6}.get(step, 3)}")
+        def turn_cold(step, pairs):
+            turned = psum.tile([P, BLOCKS, 2, P], F32, name="turned", tag=f"bank{TURN_BANKS[step]}")
             for b in range(BLOCKS):
                 for u in range(2):
-                    nc.tensor.transpose(turned[:, b, u, :], halves[b][:, u * P : (u + 1) * P], ident[:])
-            copy = nc.vector.tensor_copy if step in TURNED_ON_VECTOR else nc.scalar.copy
+                    nc.tensor.transpose(turned[:, b, u, :], pairs[b][:, u * P : (u + 1) * P], ident[:])
+            copy = nc.scalar.copy if step < TURNED_ON_SCALAR else nc.vector.tensor_copy
             copy(
-                grouped.bitcast(F32).rearrange("p (b s u) -> p b s u", s=P, u=2),
+                hidden[step].bitcast(F32).rearrange("p (b s u) -> p b s u", s=P, u=2),
                 turned[:].rearrange("p b u s -> p b s u"),
             )
 
-        def hidden_hot(step, grouped, w1h, s1h):
+        def hidden_hot(step):
             e = step - COLD
             for b in range(BLOCKS):
-                pre = psum_shared.tile([P, H], F32, name="pre", tag=f"bank{(step * BLOCKS + b) % 3 if step < E - 1 else 4 + b}")
+                pre = psum.tile([P, H], F32, name="pre", tag=first_bank(step, b))
                 for t in range(PACK):
                     cols = slice(t * P, (t + 1) * P)
                     nc.tensor.matmul_mx(
@@ -179,15 +175,13 @@ def tile_moe_hot_mlp_silu_kernel(
                         start=True, stop=True,
                     )
                 nc.scalar.activation(
-                    grouped[:, b * H : (b + 1) * H].rearrange("p (s t) -> p s t", t=PACK),
+                    hidden[step][:, b * H : (b + 1) * H].rearrange("p (s t) -> p s t", t=PACK),
                     pre[:].rearrange("p (t s) -> p s t", t=PACK),
                     SILU,
                 )
 
-        def second_layer(group, h_words, h_scales):
-            y_ps = psum_shared.tile(
-                [P, len(group) * C], F32, name="y_ps", tag=f"bank{RESULT_BANK[group[-1]]}"
-            )
+        def second_layer(number, group, h_words, h_scales):
+            y_ps = psum.tile([P, len(group) * C], F32, name="y_ps", tag=f"bank{RESULT_BANKS[number]}")
             for place, step in enumerate(group):
                 if step < COLD:
                     w2, w2_scale = w2c[:, step, :].bitcast(FP4X4), s2c[:, step, :]
@@ -199,43 +193,61 @@ def tile_moe_hot_mlp_silu_kernel(
                     rhs=h_words[:, cols].bitcast(FP8X4), rhs_scale=h_scales[:, cols], start=True, stop=True,
                 )
             first_slot = ORDER[group[0]] * C
-            copy = nc.vector.tensor_copy if group[-1] in RESULT_ON_VECTOR else nc.scalar.copy
+            copy = nc.scalar.copy if number < RESULTS_ON_SCALAR else nc.vector.tensor_copy
             copy(y[:, first_slot : first_slot + len(group) * C], y_ps[:])
 
-        for b in range(4):
-            gather_scales(1, b)
-        for b in range(4):
-            gather_words(1, b)
-        gather_words(4, 4)
+        scale_window, word_window = token_scales[:], token_words[:].bitcast(U32)
+        scales_head = keep.tile([P, P], U8, name="scales_head", tag="slot_scales", align_bytes=64)
+        scales_early = keep.tile([P, 3 * P], U8, name="scales_early", align_bytes=64)
+        words_head = keep.tile([P, P], U32, name="words_head", tag="slot_words", align_bytes=64)
+        words_early = keep.tile([P, 8 * P], U32, name="words_early", align_bytes=64)
+        gather(scales_head, 0, 0, 1, scale_window)
+        gather(scales_early, 1, 1, 3, scale_window)
+        gather(words_head, 0, 0, 1, word_window)
+        for first, blocks in [(1, 3), (4, 4), (8, 1)]:
+            gather(words_early, 1, first, blocks, word_window)
+        slot_scales = block_slices(scales_head) + block_slices(scales_early)
+        slot_words = block_slices(words_head) + block_slices(words_early)
+
         w1h = keep.tile([P, HOT, H], I32, name="w1h", align_bytes=64)
         s1h = keep.tile([P, HOT, H], U8, name="s1h", align_bytes=64)
         for e in range(HOT):
-            permute_columns(s1h[:, e, :], s1h_raw[:, e, :], 16)
             permute_columns(w1h[:, e, :], w1h_raw[:, e, :], 4)
-        hidden = [
+        for e in range(HOT):
+            permute_columns(s1h[:, e, :], s1h_raw[:, e, :], 16)
+
+        grouped = [
             keep.tile([P, len(group), PACK * C], BF16, name=f"grouped{group[0]}", align_bytes=64) for group in GROUPS
         ]
-        halves = None
-        for step in range(E):
-            waiting = halves
-            if step == 2:
-                for b, (scale_blocks, word_blocks) in enumerate([(4, 4), (4, 4), (4, 2)]):
-                    gather_scales(scale_blocks, b)
-                    gather_words(word_blocks, b)
-                gather_scales(2, 3)
+        hidden = [grouped[step // 2][:, step % 2, :] for step in range(E)]
+
+        pairs = hidden_cold(0, range(BLOCKS))
+        scales_late = keep.tile([P, 14 * P], U8, name="scales_late", tag="slot_scales", align_bytes=64)
+        words_late = keep.tile([P, 9 * P], U32, name="words_late", tag="slot_words", align_bytes=64)
+        gather(scales_late, 4, 4, 4, scale_window)
+        for first, blocks in [(8, 4), (12, 4), (16, 2)]:
+            gather(scales_late, 4, first, blocks, scale_window)
+            done = max(first, 9)
+            gather(words_late, 9, done, first + blocks - done, word_window)
+        slot_scales = slot_scales + block_slices(scales_late)
+        slot_words = slot_words + block_slices(words_late)
+
+        for step in range(1, E):
+            waiting = pairs
             if step < COLD:
-                halves = hidden_cold(step)
+                pairs = hidden_cold(step, range(BLOCKS))
             else:
-                hidden_hot(step, hidden[step // 2][:, step % 2, :], w1h, s1h)
-            if 0 < step <= COLD:
-                turn_cold(step - 1, waiting, hidden[(step - 1) // 2][:, (step - 1) % 2, :])
-        for group, grouped in zip(GROUPS, hidden):
+                hidden_hot(step)
+            if step <= COLD:
+                turn_cold(step - 1, waiting)
+
+        for number, group in enumerate(GROUPS):
             h_words = ring.tile([P, len(group) * C], U32, name="h_words", align_bytes=64)
             h_scales = ring.tile([P, len(group) * C], U8, name="h_scales", align_bytes=64)
             nc.vector.quantize_mx(
-                h_words[:].bitcast(FP8X4), h_scales[:], grouped[:].rearrange("p g x -> p (g x)")
+                h_words[:].bitcast(FP8X4), h_scales[:], grouped[number][:].rearrange("p g x -> p (g x)")
             )
-            second_layer(group, h_words, h_scales)
+            second_layer(number, group, h_words, h_scales)
 
         for chunk, (lo, hi) in enumerate(TOKEN_CHUNKS):
             width = hi - lo
@@ -250,14 +262,14 @@ def tile_moe_hot_mlp_silu_kernel(
                 sum_sb = keep.tile([P, width], F32, name=f"sum_sb{chunk}")
                 for b in range(width // P):
                     cols = slice(b * P, (b + 1) * P)
-                    sum_ps = psum_shared.tile([P, P], F32, name="sum_ps", tag=f"bank{lo // P + b}")
+                    sum_ps = psum.tile([P, P], F32, name="sum_ps", tag=f"bank{lo // P + b}")
                     for r in range(TOP):
                         nc.tensor.matmul(
                             sum_ps[:], parts[r][:, cols], ident[:],
                             start=(r == 0), stop=(r == TOP - 1), is_transpose=True,
                         )
                     nc.scalar.copy(sum_sb[:, cols], sum_ps[:])
-                back_ps = psum_shared.tile([P, width], F32, name="back_ps", tag=f"bank{5 + chunk}")
+                back_ps = psum.tile([P, width], F32, name="back_ps", tag=f"bank{BACK_BANKS[chunk]}")
                 for b in range(width // P):
                     cols = slice(b * P, (b + 1) * P)
                     nc.tensor.transpose(back_ps[:, cols], sum_sb[:, cols], ident[:])

@@ -30,13 +30,14 @@ ADD = mybir.AluOpType.add
 
 ORDER = list(range(HOT, E)) + list(range(HOT))
 GROUPS = [(0, 1), (2, 3), (4, 5), (6, 7), (8,)]
-TURNED_ON_SCALAR = 3
+TURNED = 4
+TURNED_ON_SCALAR = 2
 RESULTS_ON_SCALAR = 3
 RING = 3
 LAST_EXPERT_BANKS = (4, 5)
-TURN_BANKS = (3, 3, 3, 3, 7, 6)
+TURN_BANKS = (3, 3, 3, 7)
 RESULT_BANKS = (1, 2, 0, 3, 7)
-TOKEN_CHUNKS = [(0, 384), (384, 512), (512, 640), (640, 768)]
+TOKEN_CHUNKS = [(0, 384), (384, 512)]
 SUMMED_IN_PSUM = 2
 BACK_BANKS = (5, 6)
 
@@ -61,7 +62,7 @@ def tile_moe_hot_mlp_silu_kernel(
         w2h = keep.tile([P, HOT, PACK * N], U8, name="w2h", align_bytes=64)
         s1c_first = keep.tile([P, 2, H], U8, name="s1c_first", align_bytes=64)
         s1c_rest = keep.tile([P, COLD - 2, H], U8, name="s1c_rest", align_bytes=64)
-        s1h_raw = keep.tile([P, HOT, H], U8, name="s1h_raw", align_bytes=64)
+        s1h_raw = keep.tile([P, H], U8, name="s1h_raw", align_bytes=64)
         s2c = keep.tile([P, COLD, N], U8, name="s2c", align_bytes=64)
         s2h = keep.tile([P, HOT, N], U8, name="s2h", align_bytes=64)
         gate_sb = keep.tile([P, TOP, T], F32, name="gate_sb")
@@ -99,9 +100,13 @@ def tile_moe_hot_mlp_silu_kernel(
         load_scales(s1c_first, w1c_scales[:2])
         load_words(w1c[1], w1c_words[2:4, 0])
         load_scales(s1c_rest, w1c_scales[2:])
-        nc.sync.dma_start(w1h_raw[:], w1h_words[:, 0].rearrange("e p i d -> p e (i d)").bitcast(I32))
         load_words(w1c[2], w1c_words[4:6, 0])
-        load_scales(s1h_raw, w1h_scales)
+        nc.sync.dma_start(w1h_raw[:], w1h_words[:, 0].rearrange("e p i d -> p e (i d)").bitcast(I32))
+        for q in range(QUADRANTS):
+            nc.sync.dma_start(
+                s1h_raw[QUADRANT * q : QUADRANT * q + HOT * QUADRANT_ROWS, :].bitcast(I32),
+                w1h_scales[:, 0, QUADRANT_ROWS * q : QUADRANT_ROWS * (q + 1), :].bitcast(I32),
+            )
         load_words(w2c, w2c_words[:, 0])
         load_scales(s2c, w2c_scales)
         load_words(w2h, w2h_words[:, 0].rearrange("e p n d -> e p (n d)"))
@@ -119,10 +124,9 @@ def tile_moe_hot_mlp_silu_kernel(
         def block_slices(tile):
             return [tile[:, column : column + P] for column in range(0, tile.shape[1], P)]
 
-        def permute_columns(dst, src, run):
+        def permute_columns(dst, src):
             nc.gpsimd.tensor_copy(
-                dst.rearrange("p (t c i) -> p c t i", t=PACK, i=run),
-                src.rearrange("p (c i t) -> p c t i", t=PACK, i=run),
+                dst.rearrange("p (t m) -> p t m", t=PACK), src.rearrange("p (m t) -> p t m", t=PACK)
             )
 
         def first_bank(step, b):
@@ -161,15 +165,16 @@ def tile_moe_hot_mlp_silu_kernel(
             )
 
         def hidden_hot(step):
-            e = step - COLD
+            w1, w1_scale = permuted[step]
+            word = w1.shape[1] // H
             for b in range(BLOCKS):
                 pre = psum.tile([P, H], F32, name="pre", tag=first_bank(step, b))
                 for t in range(PACK):
                     cols = slice(t * P, (t + 1) * P)
                     nc.tensor.matmul_mx(
                         pre[:, cols],
-                        lhsT=w1h[:, e, cols].bitcast(FP8X4),
-                        lhsT_scale=s1h[:, e, cols],
+                        lhsT=w1[:, word * t * P : word * (t + 1) * P].bitcast(FP4X4 if step < COLD else FP8X4),
+                        lhsT_scale=w1_scale[:, cols],
                         rhs=slot_words[step * BLOCKS + b].bitcast(FP8X4),
                         rhs_scale=slot_scales[step * BLOCKS + b],
                         start=True, stop=True,
@@ -209,12 +214,20 @@ def tile_moe_hot_mlp_silu_kernel(
         slot_scales = block_slices(scales_head) + block_slices(scales_early)
         slot_words = block_slices(words_head) + block_slices(words_early)
 
-        w1h = keep.tile([P, HOT, H], I32, name="w1h", align_bytes=64)
-        s1h = keep.tile([P, HOT, H], U8, name="s1h", align_bytes=64)
-        for e in range(HOT):
-            permute_columns(w1h[:, e, :], w1h_raw[:, e, :], 4)
-        for e in range(HOT):
-            permute_columns(s1h[:, e, :], s1h_raw[:, e, :], 16)
+        permuted = {}
+        for step in range(TURNED, E):
+            cold = step < COLD
+            w1 = keep.tile([P, (2 if cold else PACK) * H], U8, name=f"w1_permuted{step}", align_bytes=64)
+            if step <= COLD:
+                w1_scale = keep.tile([P, H], U8, name=f"s1_permuted{step}", align_bytes=64)
+            if cold:
+                permute_columns(w1[:].bitcast(U16), w1c[step // 2][:, step % 2, :].bitcast(U16))
+                permute_columns(w1_scale[:], s1c_rest[:, step - 2, :])
+            else:
+                permute_columns(w1[:].bitcast(I32), w1h_raw[:, step - COLD, :])
+                if step == COLD:
+                    permute_columns(w1_scale[:], s1h_raw[:])
+            permuted[step] = (w1[:], w1_scale[QUADRANT_ROWS * max(step - COLD, 0) :, :])
 
         grouped = [
             keep.tile([P, len(group), PACK * C], BF16, name=f"grouped{group[0]}", align_bytes=64) for group in GROUPS
@@ -234,11 +247,11 @@ def tile_moe_hot_mlp_silu_kernel(
 
         for step in range(1, E):
             waiting = pairs
-            if step < COLD:
+            if step < TURNED:
                 pairs = hidden_cold(step, range(BLOCKS))
             else:
                 hidden_hot(step)
-            if step <= COLD:
+            if step <= TURNED:
                 turn_cold(step - 1, waiting)
 
         for number, group in enumerate(GROUPS):
@@ -275,8 +288,21 @@ def tile_moe_hot_mlp_silu_kernel(
                     nc.tensor.transpose(back_ps[:, cols], sum_sb[:, cols], ident[:])
                 nc.scalar.copy(total[:], back_ps[:])
                 nc.scalar.dma_start(out[:, lo:hi], total[:])
-            else:
-                pair = keep.tile([P, width], F32, name=f"pair{chunk}")
-                nc.vector.tensor_tensor(pair[:], parts[0][:], parts[1][:], ADD)
-                nc.vector.tensor_tensor(total[:], pair[:], parts[2][:], ADD)
-                nc.sync.dma_start(out[:, lo:hi], total[:])
+
+        first = TOKEN_CHUNKS[-1][1]
+
+        def gated(r, lo, hi):
+            part = keep.tile([P, hi - lo], F32, name=f"part{r}_{lo}")
+            entries = pos_sb[r][:, lo // LIST_ROWS : hi // LIST_ROWS]
+            nc.vector.tensor_tensor(part[:], y[:].indirect(entries), gate_sb[:, r, lo:hi], MULT)
+            return part
+
+        parts = [gated(r, first, T) for r in range(TOP - 1)]
+        last = [gated(TOP - 1, first, first + P)]
+        pair = keep.tile([P, T - first], F32, name="pair")
+        nc.vector.tensor_tensor(pair[:], parts[0][:], parts[1][:], ADD)
+        last.append(gated(TOP - 1, first + P, T))
+        for b in range(2):
+            total = keep.tile([P, P], F32, name=f"total_last{b}")
+            nc.vector.tensor_tensor(total[:], pair[:, b * P : (b + 1) * P], last[b][:], ADD)
+            nc.sync.dma_start(out[:, first + b * P : first + (b + 1) * P], total[:])

@@ -30,13 +30,15 @@ ADD = mybir.AluOpType.add
 
 ORDER = list(range(HOT, E)) + list(range(HOT))
 GROUPS = [(0, 1), (2, 3), (4, 5), (6, 7), (8,)]
-TURNED = 4
-TURNED_ON_SCALAR = 2
-RESULTS_ON_SCALAR = 3
+TURNED = 2
+TURNED_ON_SCALAR = 1
+RESULTS_ON_SCALAR = (0, 1, 2)
+SHIFTED = 112
 RING = 3
 LAST_EXPERT_BANKS = (4, 5)
-TURN_BANKS = (3, 3, 3, 7)
-RESULT_BANKS = (1, 2, 0, 3, 7)
+TURN_BANKS = (3, 7)
+RESULT_BANKS = (2, 1, 0, 3, 6)
+OWN_BANKS = {9: 7}
 TOKEN_CHUNKS = [(0, 384), (384, 512)]
 SUMMED_IN_PSUM = 2
 BACK_BANKS = (5, 6)
@@ -56,12 +58,16 @@ def tile_moe_hot_mlp_silu_kernel(
         pos_sb = [keep.tile([P, T // LIST_ROWS], U16, name=f"pos_sb{r}") for r in range(TOP)]
         token_words = keep.tile([P, T], I32, name="token_words", align_bytes=64)
         token_scales = keep.tile([P, T], U8, name="token_scales", align_bytes=64)
-        w1c = [keep.tile([P, 2, 2 * H], U8, name=f"w1c{a}", align_bytes=64) for a in range(COLD // 2)]
+        w1c_first = keep.tile([P, TURNED, 2 * H], U8, name="w1c_first", align_bytes=64)
+        w1c_raw = keep.tile([P, COLD - TURNED, 2 * H], U8, name="w1c_raw", align_bytes=64)
         w1h_raw = keep.tile([P, HOT, H], I32, name="w1h_raw", align_bytes=64)
         w2c = keep.tile([P, COLD, 2 * N], U8, name="w2c", align_bytes=64)
         w2h = keep.tile([P, HOT, PACK * N], U8, name="w2h", align_bytes=64)
         s1c_first = keep.tile([P, 2, H], U8, name="s1c_first", align_bytes=64)
-        s1c_rest = keep.tile([P, COLD - 2, H], U8, name="s1c_rest", align_bytes=64)
+        s1c_raw = keep.tile([P, H], U8, name="s1c_raw", align_bytes=64)
+        s1c_shifted = [
+            keep.tile([P, H], U8, name=f"s1c_shifted{a}", align_bytes=64) for a in range(COLD - TURNED - 1)
+        ]
         s1h_raw = keep.tile([P, H], U8, name="s1h_raw", align_bytes=64)
         s2c = keep.tile([P, COLD, N], U8, name="s2c", align_bytes=64)
         s2h = keep.tile([P, HOT, N], U8, name="s2h", align_bytes=64)
@@ -71,20 +77,35 @@ def tile_moe_hot_mlp_silu_kernel(
         warm_in = keep.tile([P, 8], F32, name="warm_in")
         warm_out = keep.tile([P, 8], F32, name="warm_out")
 
+        nc.gpsimd.dma_start(
+            w1c_first[:].bitcast(I32), w1c_words[:TURNED, 0].rearrange("e p b -> p e b").bitcast(I32)
+        )
         nc.vector.memset(warm_in[:], 0.0)
-        for plane in (s1c_first, s1c_rest, s2c, s1h_raw, s2h):
+        for plane in (s1c_first, s1c_raw, *s1c_shifted, s1h_raw, s2c, s2h):
             nc.vector.memset(plane[:].bitcast(I32), 0)
         make_identity(nc, ident[:])
 
         def load_words(tile, words):
             nc.sync.dma_start(tile[:].bitcast(I32), words.rearrange("e p b -> p e b").bitcast(I32))
 
-        def load_scales(plane, scales):
-            for j in range(QUADRANT_ROWS):
+        def load_scales(plane, scales, rows=range(QUADRANT_ROWS)):
+            for j in rows:
                 nc.sync.dma_start(
                     plane[j:P:QUADRANT].bitcast(I32),
                     scales[:, 0, j::QUADRANT_ROWS, :].rearrange("e q i -> q e i").bitcast(I32),
                 )
+
+        def load_stacked(plane, scales, place=0):
+            for q in range(QUADRANTS):
+                nc.sync.dma_start(
+                    plane[QUADRANT * q + QUADRANT_ROWS * place :][: scales.shape[0] * QUADRANT_ROWS, :].bitcast(I32),
+                    scales[:, 0, QUADRANT_ROWS * q : QUADRANT_ROWS * (q + 1), :].bitcast(I32),
+                )
+
+        def permute_columns(dst, src):
+            nc.gpsimd.tensor_copy(
+                dst.rearrange("p (t m) -> p t m", t=PACK), src.rearrange("p (m t) -> p t m", t=PACK)
+            )
 
         for q in range(QUADRANTS):
             queue = nc.sync if q < QUADRANTS // 2 else nc.scalar
@@ -94,19 +115,22 @@ def tile_moe_hot_mlp_silu_kernel(
                 rows.unsqueeze(0).broadcast_to([QUADRANT // QUADRANT_ROWS, QUADRANT_ROWS, T // 4]),
             )
         nc.sync.dma_start(offs_sb[:], offs)
+        load_scales(s1c_first, w1c_scales[:TURNED], (0, 1))
         nc.sync.dma_start(token_words[:], x_words[0].rearrange("p t d -> p (t d)").bitcast(I32))
         nc.scalar.activation(warm_out[:], warm_in[:], SILU)
-        load_words(w1c[0], w1c_words[0:2, 0])
-        load_scales(s1c_first, w1c_scales[:2])
-        load_words(w1c[1], w1c_words[2:4, 0])
-        load_scales(s1c_rest, w1c_scales[2:])
-        load_words(w1c[2], w1c_words[4:6, 0])
+        load_scales(s1c_first, w1c_scales[:TURNED], (2, 3))
+        load_stacked(s1c_raw, w1c_scales[TURNED:])
+        load_words(w1c_raw, w1c_words[TURNED:, 0])
         nc.sync.dma_start(w1h_raw[:], w1h_words[:, 0].rearrange("e p i d -> p e (i d)").bitcast(I32))
-        for q in range(QUADRANTS):
+        load_stacked(s1h_raw, w1h_scales[:2])
+        s1c_stacked = keep.tile([P, H], U8, name="s1c_stacked", align_bytes=64)
+        permute_columns(s1c_stacked[:], s1c_raw[:])
+        for a in range(1, COLD - TURNED):
             nc.sync.dma_start(
-                s1h_raw[QUADRANT * q : QUADRANT * q + HOT * QUADRANT_ROWS, :].bitcast(I32),
-                w1h_scales[:, 0, QUADRANT_ROWS * q : QUADRANT_ROWS * (q + 1), :].bitcast(I32),
+                s1c_shifted[a - 1][:SHIFTED, :].bitcast(I32),
+                s1c_stacked[QUADRANT_ROWS * a : QUADRANT_ROWS * a + SHIFTED, :].bitcast(I32),
             )
+        load_stacked(s1h_raw, w1h_scales[2:], 2)
         load_words(w2c, w2c_words[:, 0])
         load_scales(s2c, w2c_scales)
         load_words(w2h, w2h_words[:, 0].rearrange("e p n d -> e p (n d)"))
@@ -124,17 +148,15 @@ def tile_moe_hot_mlp_silu_kernel(
         def block_slices(tile):
             return [tile[:, column : column + P] for column in range(0, tile.shape[1], P)]
 
-        def permute_columns(dst, src):
-            nc.gpsimd.tensor_copy(
-                dst.rearrange("p (t m) -> p t m", t=PACK), src.rearrange("p (m t) -> p t m", t=PACK)
-            )
-
         def first_bank(step, b):
-            return f"bank{(step * BLOCKS + b) % RING if step < E - 1 else LAST_EXPERT_BANKS[b]}"
+            block = step * BLOCKS + b
+            if block in OWN_BANKS:
+                return f"bank{OWN_BANKS[block]}"
+            return f"bank{block % RING if step < E - 1 else LAST_EXPERT_BANKS[b]}"
 
         def hidden_cold(step, blocks):
-            w1 = w1c[step // 2][:, step % 2, :].bitcast(FP4X4)
-            w1_scale = s1c_first[:, step, :] if step < 2 else s1c_rest[:, step - 2, :]
+            w1 = w1c_first[:, step, :].bitcast(FP4X4)
+            w1_scale = s1c_first[:, step, :]
             pairs = []
             for b in blocks:
                 pre = psum.tile([P, H], F32, name="pre", tag=first_bank(step, b))
@@ -198,7 +220,7 @@ def tile_moe_hot_mlp_silu_kernel(
                     rhs=h_words[:, cols].bitcast(FP8X4), rhs_scale=h_scales[:, cols], start=True, stop=True,
                 )
             first_slot = ORDER[group[0]] * C
-            copy = nc.scalar.copy if number < RESULTS_ON_SCALAR else nc.vector.tensor_copy
+            copy = nc.scalar.copy if number in RESULTS_ON_SCALAR else nc.vector.tensor_copy
             copy(y[:, first_slot : first_slot + len(group) * C], y_ps[:])
 
         scale_window, word_window = token_scales[:], token_words[:].bitcast(U32)
@@ -218,16 +240,16 @@ def tile_moe_hot_mlp_silu_kernel(
         for step in range(TURNED, E):
             cold = step < COLD
             w1 = keep.tile([P, (2 if cold else PACK) * H], U8, name=f"w1_permuted{step}", align_bytes=64)
-            if step <= COLD:
-                w1_scale = keep.tile([P, H], U8, name=f"s1_permuted{step}", align_bytes=64)
             if cold:
-                permute_columns(w1[:].bitcast(U16), w1c[step // 2][:, step % 2, :].bitcast(U16))
-                permute_columns(w1_scale[:], s1c_rest[:, step - 2, :])
+                permute_columns(w1[:].bitcast(U16), w1c_raw[:, step - TURNED, :].bitcast(U16))
+                w1_scale = s1c_stacked[:] if step == TURNED else s1c_shifted[step - TURNED - 1][:]
             else:
                 permute_columns(w1[:].bitcast(I32), w1h_raw[:, step - COLD, :])
                 if step == COLD:
-                    permute_columns(w1_scale[:], s1h_raw[:])
-            permuted[step] = (w1[:], w1_scale[QUADRANT_ROWS * max(step - COLD, 0) :, :])
+                    s1h = keep.tile([P, H], U8, name="s1h", align_bytes=64)
+                    permute_columns(s1h[:], s1h_raw[:])
+                w1_scale = s1h[QUADRANT_ROWS * (step - COLD) :, :]
+            permuted[step] = (w1[:], w1_scale)
 
         grouped = [
             keep.tile([P, len(group), PACK * C], BF16, name=f"grouped{group[0]}", align_bytes=64) for group in GROUPS
@@ -251,10 +273,13 @@ def tile_moe_hot_mlp_silu_kernel(
                 pairs = hidden_cold(step, range(BLOCKS))
             else:
                 hidden_hot(step)
-            if step <= TURNED:
-                turn_cold(step - 1, waiting)
+            if step == 1:
+                turn_cold(0, waiting)
+            if step == 4:
+                turn_cold(1, pairs)
 
-        for number, group in enumerate(GROUPS):
+        for number in (1, 0, 2, 3, 4):
+            group = GROUPS[number]
             h_words = ring.tile([P, len(group) * C], U32, name="h_words", align_bytes=64)
             h_scales = ring.tile([P, len(group) * C], U8, name="h_scales", align_bytes=64)
             nc.vector.quantize_mx(

@@ -81,8 +81,10 @@ def tile_moe_hot_mlp_silu_kernel(
             w1c_first[:].bitcast(I32), w1c_words[:TURNED, 0].rearrange("e p b -> p e b").bitcast(I32)
         )
         nc.vector.memset(warm_in[:], 0.0)
-        for plane in (s1c_first, s1c_raw, *s1c_shifted, s1h_raw, s2c, s2h):
+        for plane in (s1c_first, s1c_raw):
             nc.vector.memset(plane[:].bitcast(I32), 0)
+        for plane in (s1h_raw, *s1c_shifted, s2c, s2h):
+            nc.gpsimd.memset(plane[:].bitcast(I32), 0)
         make_identity(nc, ident[:])
 
         def load_words(tile, words):
@@ -287,47 +289,43 @@ def tile_moe_hot_mlp_silu_kernel(
             )
             second_layer(number, group, h_words, h_scales)
 
-        for chunk, (lo, hi) in enumerate(TOKEN_CHUNKS):
-            width = hi - lo
-            parts = []
-            for r in range(TOP):
-                part = keep.tile([P, width], F32, name=f"part{r}_{chunk}")
-                entries = pos_sb[r][:, lo // LIST_ROWS : hi // LIST_ROWS]
-                nc.vector.tensor_tensor(part[:], y[:].indirect(entries), gate_sb[:, r, lo:hi], MULT)
-                parts.append(part)
-            total = keep.tile([P, width], F32, name=f"total{chunk}")
-            if chunk < SUMMED_IN_PSUM:
-                sum_sb = keep.tile([P, width], F32, name=f"sum_sb{chunk}")
-                for b in range(width // P):
-                    cols = slice(b * P, (b + 1) * P)
-                    sum_ps = psum.tile([P, P], F32, name="sum_ps", tag=f"bank{lo // P + b}")
-                    for r in range(TOP):
-                        nc.tensor.matmul(
-                            sum_ps[:], parts[r][:, cols], ident[:],
-                            start=(r == 0), stop=(r == TOP - 1), is_transpose=True,
-                        )
-                    nc.scalar.copy(sum_sb[:, cols], sum_ps[:])
-                back_ps = psum.tile([P, width], F32, name="back_ps", tag=f"bank{BACK_BANKS[chunk]}")
-                for b in range(width // P):
-                    cols = slice(b * P, (b + 1) * P)
-                    nc.tensor.transpose(back_ps[:, cols], sum_sb[:, cols], ident[:])
-                nc.scalar.copy(total[:], back_ps[:])
-                nc.scalar.dma_start(out[:, lo:hi], total[:])
-
-        first = TOKEN_CHUNKS[-1][1]
+        parts = [keep.tile([P, T], F32, name=f"part{r}") for r in range(TOP)]
 
         def gated(r, lo, hi):
-            part = keep.tile([P, hi - lo], F32, name=f"part{r}_{lo}")
             entries = pos_sb[r][:, lo // LIST_ROWS : hi // LIST_ROWS]
-            nc.vector.tensor_tensor(part[:], y[:].indirect(entries), gate_sb[:, r, lo:hi], MULT)
-            return part
+            nc.vector.tensor_tensor(parts[r][:, lo:hi], y[:].indirect(entries), gate_sb[:, r, lo:hi], MULT)
 
-        parts = [gated(r, first, T) for r in range(TOP - 1)]
-        last = [gated(TOP - 1, first, first + P)]
+        def sum_in_psum(chunk):
+            lo, hi = TOKEN_CHUNKS[chunk]
+            sum_sb = keep.tile([P, hi - lo], F32, name=f"sum_sb{chunk}")
+            for column in range(lo, hi, P):
+                sum_ps = psum.tile([P, P], F32, name="sum_ps", tag=f"bank{column // P}")
+                for r in range(TOP):
+                    nc.tensor.matmul(
+                        sum_ps[:], parts[r][:, column : column + P], ident[:],
+                        start=(r == 0), stop=(r == TOP - 1), is_transpose=True,
+                    )
+                nc.scalar.copy(sum_sb[:, column - lo : column - lo + P], sum_ps[:])
+            back_ps = psum.tile([P, hi - lo], F32, name="back_ps", tag=f"bank{BACK_BANKS[chunk]}")
+            for column in range(0, hi - lo, P):
+                nc.tensor.transpose(back_ps[:, column : column + P], sum_sb[:, column : column + P], ident[:])
+            total = keep.tile([P, hi - lo], F32, name=f"total{chunk}")
+            nc.scalar.copy(total[:], back_ps[:])
+            nc.scalar.dma_start(out[:, lo:hi], total[:])
+
+        first = TOKEN_CHUNKS[-1][1]
+        for r in range(TOP - 1):
+            gated(r, 0, first)
+        for chunk, (lo, hi) in enumerate(TOKEN_CHUNKS):
+            gated(TOP - 1, lo, hi)
+            sum_in_psum(chunk)
+        for r in range(TOP - 1):
+            gated(r, first, T)
         pair = keep.tile([P, T - first], F32, name="pair")
-        nc.vector.tensor_tensor(pair[:], parts[0][:], parts[1][:], ADD)
-        last.append(gated(TOP - 1, first + P, T))
-        for b in range(2):
-            total = keep.tile([P, P], F32, name=f"total_last{b}")
-            nc.vector.tensor_tensor(total[:], pair[:, b * P : (b + 1) * P], last[b][:], ADD)
-            nc.sync.dma_start(out[:, first + b * P : first + (b + 1) * P], total[:])
+        gated(TOP - 1, first, first + P)
+        nc.vector.tensor_tensor(pair[:], parts[0][:, first:], parts[1][:, first:], ADD)
+        gated(TOP - 1, first + P, T)
+        for lo in range(first, T, P):
+            total = keep.tile([P, P], F32, name=f"total_last{lo}")
+            nc.vector.tensor_tensor(total[:], pair[:, lo - first : lo - first + P], parts[TOP - 1][:, lo : lo + P], ADD)
+            nc.sync.dma_start(out[:, lo : lo + P], total[:])

@@ -135,11 +135,11 @@ def tile_moe_hot_mlp_silu_kernel(
         load_stacked(s1h_raw, w1h_scales[2:], 2)
         load_words(w2c, w2c_words[:, 0])
         load_scales(s2c, w2c_scales)
+        nc.sync.dma_start(gate_sb[:], gate.rearrange("r p t -> p r t"))
         load_words(w2h, w2h_words[:, 0].rearrange("e p n d -> e p (n d)"))
         load_scales(s2h, w2h_scales)
         for r, pos in enumerate((pos1, pos2, pos3)):
             nc.sync.dma_start(pos_sb[r][:], pos)
-        nc.sync.dma_start(gate_sb[:], gate.rearrange("r p t -> p r t"))
 
         def gather(tile, tile_first, first, blocks, window):
             slot = ORDER[first // BLOCKS] * C + first % BLOCKS * P

@@ -104,9 +104,10 @@ def tile_moe_hot_mlp_silu_kernel(
                     scales[:, 0, QUADRANT_ROWS * q : QUADRANT_ROWS * (q + 1), :].bitcast(I32),
                 )
 
-        def permute_columns(dst, src):
+        def permute_columns(dst, src, line):
             nc.gpsimd.tensor_copy(
-                dst.rearrange("p (t m) -> p t m", t=PACK), src.rearrange("p (m t) -> p t m", t=PACK)
+                dst.rearrange("p (t a m) -> p a t m", t=PACK, m=line),
+                src.rearrange("p (a m t) -> p a t m", t=PACK, m=line),
             )
 
         for q in range(QUADRANTS):
@@ -126,7 +127,7 @@ def tile_moe_hot_mlp_silu_kernel(
         nc.sync.dma_start(w1h_raw[:], w1h_words[:, 0].rearrange("e p i d -> p e (i d)").bitcast(I32))
         load_stacked(s1h_raw, w1h_scales[:2])
         s1c_stacked = keep.tile([P, H], U8, name="s1c_stacked", align_bytes=64)
-        permute_columns(s1c_stacked[:], s1c_raw[:])
+        permute_columns(s1c_stacked[:], s1c_raw[:], 16)
         for a in range(1, COLD - TURNED):
             nc.sync.dma_start(
                 s1c_shifted[a - 1][:SHIFTED, :].bitcast(I32),
@@ -243,13 +244,13 @@ def tile_moe_hot_mlp_silu_kernel(
             cold = step < COLD
             w1 = keep.tile([P, (2 if cold else PACK) * H], U8, name=f"w1_permuted{step}", align_bytes=64)
             if cold:
-                permute_columns(w1[:].bitcast(U16), w1c_raw[:, step - TURNED, :].bitcast(U16))
+                permute_columns(w1[:].bitcast(U16), w1c_raw[:, step - TURNED, :].bitcast(U16), 8)
                 w1_scale = s1c_stacked[:] if step == TURNED else s1c_shifted[step - TURNED - 1][:]
             else:
-                permute_columns(w1[:].bitcast(I32), w1h_raw[:, step - COLD, :])
+                permute_columns(w1[:].bitcast(I32), w1h_raw[:, step - COLD, :], 4)
                 if step == COLD:
                     s1h = keep.tile([P, H], U8, name="s1h", align_bytes=64)
-                    permute_columns(s1h[:], s1h_raw[:])
+                    permute_columns(s1h[:], s1h_raw[:], 16)
                 w1_scale = s1h[QUADRANT_ROWS * (step - COLD) :, :]
             permuted[step] = (w1[:], w1_scale)
 

@@ -28,16 +28,17 @@ SILU = mybir.ActivationFunctionType.Silu
 MULT = mybir.AluOpType.mult
 ADD = mybir.AluOpType.add
 
-ORDER = list(range(HOT, E)) + list(range(HOT))
+ORDER = [3, 4, 7, 8, 5, 6, 0, 1, 2]
+WORK = [0, 1, 3, 2, 5, 4, 6, 7, 8]
 GROUPS = [(0, 1), (2, 3), (4, 5), (6, 7), (8,)]
 TURNED = 2
-TURNED_ON_SCALAR = 1
-RESULTS_ON_SCALAR = (0, 1, 2)
+TURNED_ON_SCALAR = 0
+RESULTS_ON_SCALAR = (0, 1, 3)
 SHIFTED = 112
 RING = 3
 LAST_EXPERT_BANKS = (4, 5)
-TURN_BANKS = (3, 7)
-RESULT_BANKS = (2, 1, 0, 3, 6)
+TURN_BANKS = (7,)
+RESULT_BANKS = (2, 1, 5, 3, 6)
 OWN_BANKS = {9: 7}
 TOKEN_CHUNKS = [(0, 384), (384, 512)]
 SUMMED_IN_PSUM = 2
@@ -118,17 +119,19 @@ def tile_moe_hot_mlp_silu_kernel(
                 rows.unsqueeze(0).broadcast_to([QUADRANT // QUADRANT_ROWS, QUADRANT_ROWS, T // 4]),
             )
         nc.sync.dma_start(offs_sb[:], offs)
-        load_scales(s1c_first, w1c_scales[:TURNED], (0, 1))
+        load_scales(s1c_first, w1c_scales[:: COLD - 1], (0, 1))
         nc.sync.dma_start(token_words[:], x_words[0].rearrange("p t d -> p (t d)").bitcast(I32))
         nc.scalar.activation(warm_out[:], warm_in[:], SILU)
-        load_scales(s1c_first, w1c_scales[:TURNED], (2, 3))
-        load_stacked(s1c_raw, w1c_scales[TURNED:])
+        load_scales(s1c_first, w1c_scales[:: COLD - 1], (2, 3))
+        load_stacked(s1c_raw, w1c_scales[1 : COLD - 1])
         load_words(w1c_raw, w1c_words[TURNED:, 0])
         nc.sync.dma_start(w1h_raw[:], w1h_words[:, 0].rearrange("e p i d -> p e (i d)").bitcast(I32))
         load_stacked(s1h_raw, w1h_scales[:2])
+        w1c_second = keep.tile([P, 2 * H], U8, name="w1c_second", align_bytes=64)
+        permute_columns(w1c_second[:].bitcast(U16), w1c_first[:, 1, :].bitcast(U16), 8)
         s1c_stacked = keep.tile([P, H], U8, name="s1c_stacked", align_bytes=64)
         permute_columns(s1c_stacked[:], s1c_raw[:], 16)
-        for a in range(1, COLD - TURNED):
+        for a in (3, 2, 1):
             nc.sync.dma_start(
                 s1c_shifted[a - 1][:SHIFTED, :].bitcast(I32),
                 s1c_stacked[QUADRANT_ROWS * a : QUADRANT_ROWS * a + SHIFTED, :].bitcast(I32),
@@ -142,17 +145,14 @@ def tile_moe_hot_mlp_silu_kernel(
         for r, pos in enumerate((pos1, pos2, pos3)):
             nc.sync.dma_start(pos_sb[r][:], pos)
 
-        def gather(tile, tile_first, first, blocks, window):
-            slot = ORDER[first // BLOCKS] * C + first % BLOCKS * P
-            entries = offs_sb[:, slot // LIST_ROWS : (slot + blocks * P) // LIST_ROWS]
-            column = (first - tile_first) * P
-            nc.vector.tensor_copy(tile[:, column : column + blocks * P], window.indirect(entries))
-
-        def block_slices(tile):
-            return [tile[:, column : column + P] for column in range(0, tile.shape[1], P)]
+        def gather(tile, column, first, blocks, window, gathered):
+            entries = offs_sb[:, first * P // LIST_ROWS : (first + blocks) * P // LIST_ROWS]
+            nc.vector.tensor_copy(tile[:, column * P : (column + blocks) * P], window.indirect(entries))
+            for b in range(blocks):
+                gathered[first + b] = tile[:, (column + b) * P : (column + b + 1) * P]
 
         def first_bank(step, b):
-            block = step * BLOCKS + b
+            block = WORK.index(step) * BLOCKS + b
             if block in OWN_BANKS:
                 return f"bank{OWN_BANKS[block]}"
             return f"bank{block % RING if step < E - 1 else LAST_EXPERT_BANKS[b]}"
@@ -165,8 +165,8 @@ def tile_moe_hot_mlp_silu_kernel(
                 pre = psum.tile([P, H], F32, name="pre", tag=first_bank(step, b))
                 nc.tensor.matmul_mx(
                     pre[:],
-                    lhsT=slot_words[step * BLOCKS + b].bitcast(FP8X4),
-                    lhsT_scale=slot_scales[step * BLOCKS + b],
+                    lhsT=slot_words[ORDER[step] * BLOCKS + b].bitcast(FP8X4),
+                    lhsT_scale=slot_scales[ORDER[step] * BLOCKS + b],
                     rhs=w1, rhs_scale=w1_scale, start=True, stop=True,
                 )
                 h = ring.tile([P, H], BF16, name="h")
@@ -200,13 +200,13 @@ def tile_moe_hot_mlp_silu_kernel(
                         pre[:, cols],
                         lhsT=w1[:, word * t * P : word * (t + 1) * P].bitcast(FP4X4 if step < COLD else FP8X4),
                         lhsT_scale=w1_scale[:, cols],
-                        rhs=slot_words[step * BLOCKS + b].bitcast(FP8X4),
-                        rhs_scale=slot_scales[step * BLOCKS + b],
+                        rhs=slot_words[ORDER[step] * BLOCKS + b].bitcast(FP8X4),
+                        rhs_scale=slot_scales[ORDER[step] * BLOCKS + b],
                         start=True, stop=True,
                     )
                 nc.scalar.activation(
-                    hidden[step][:, b * H : (b + 1) * H].rearrange("p (s t) -> p s t", t=PACK),
-                    pre[:].rearrange("p (t s) -> p s t", t=PACK),
+                    hidden[step][:, b * H : (b + 1) * H].rearrange("p (c s t) -> p c t s", t=PACK, s=2),
+                    pre[:].rearrange("p (t c s) -> p c t s", t=PACK, s=2),
                     SILU,
                 )
 
@@ -214,7 +214,8 @@ def tile_moe_hot_mlp_silu_kernel(
             y_ps = psum.tile([P, len(group) * C], F32, name="y_ps", tag=f"bank{RESULT_BANKS[number]}")
             for place, step in enumerate(group):
                 if step < COLD:
-                    w2, w2_scale = w2c[:, step, :].bitcast(FP4X4), s2c[:, step, :]
+                    f = ORDER[step] - HOT
+                    w2, w2_scale = w2c[:, f, :].bitcast(FP4X4), s2c[:, f, :]
                 else:
                     w2, w2_scale = w2h[:, step - COLD, :].bitcast(FP8X4), s2h[:, step - COLD, :]
                 cols = slice(place * C, (place + 1) * C)
@@ -230,22 +231,25 @@ def tile_moe_hot_mlp_silu_kernel(
         scales_head = keep.tile([P, P], U8, name="scales_head", tag="slot_scales", align_bytes=64)
         scales_early = keep.tile([P, 3 * P], U8, name="scales_early", align_bytes=64)
         words_head = keep.tile([P, P], U32, name="words_head", tag="slot_words", align_bytes=64)
-        words_early = keep.tile([P, 8 * P], U32, name="words_early", align_bytes=64)
-        gather(scales_head, 0, 0, 1, scale_window)
-        gather(scales_early, 1, 1, 3, scale_window)
-        gather(words_head, 0, 0, 1, word_window)
-        for first, blocks in [(1, 3), (4, 4), (8, 1)]:
-            gather(words_early, 1, first, blocks, word_window)
-        slot_scales = block_slices(scales_head) + block_slices(scales_early)
-        slot_words = block_slices(words_head) + block_slices(words_early)
+        words_early = keep.tile([P, 5 * P], U32, name="words_early", align_bytes=64)
+        slot_scales, slot_words = {}, {}
+        gather(scales_head, 0, 6, 1, scale_window, slot_scales)
+        gather(scales_early, 0, 7, 3, scale_window, slot_scales)
+        gather(words_head, 0, 6, 1, word_window, slot_words)
+        gather(words_early, 0, 7, 3, word_window, slot_words)
+        gather(words_early, 3, 16, 2, word_window, slot_words)
 
-        permuted = {}
-        for step in range(TURNED, E):
+        permuted = {1: (w1c_second[:], s1c_stacked[:])}
+        for step in WORK[2:]:
             cold = step < COLD
             w1 = keep.tile([P, (2 if cold else PACK) * H], U8, name=f"w1_permuted{step}", align_bytes=64)
             if cold:
-                permute_columns(w1[:].bitcast(U16), w1c_raw[:, step - TURNED, :].bitcast(U16), 8)
-                w1_scale = s1c_stacked[:] if step == TURNED else s1c_shifted[step - TURNED - 1][:]
+                f = ORDER[step] - HOT
+                if f == COLD - 1:
+                    s1c_last = keep.tile([P, H], U8, name="s1c_last", align_bytes=64)
+                    permute_columns(s1c_last[:], s1c_first[:, 1, :], 16)
+                permute_columns(w1[:].bitcast(U16), w1c_raw[:, f - TURNED, :].bitcast(U16), 8)
+                w1_scale = s1c_last[:] if f == COLD - 1 else s1c_shifted[f - TURNED][:]
             else:
                 permute_columns(w1[:].bitcast(I32), w1h_raw[:, step - COLD, :], 4)
                 if step == COLD:
@@ -261,25 +265,20 @@ def tile_moe_hot_mlp_silu_kernel(
 
         pairs = hidden_cold(0, range(BLOCKS))
         scales_late = keep.tile([P, 14 * P], U8, name="scales_late", tag="slot_scales", align_bytes=64)
-        words_late = keep.tile([P, 9 * P], U32, name="words_late", tag="slot_words", align_bytes=64)
-        gather(scales_late, 4, 4, 4, scale_window)
-        for first, blocks in [(8, 4), (12, 4), (16, 2)]:
-            gather(scales_late, 4, first, blocks, scale_window)
-            done = max(first, 9)
-            gather(words_late, 9, done, first + blocks - done, word_window)
-        slot_scales = slot_scales + block_slices(scales_late)
-        slot_words = slot_words + block_slices(words_late)
+        words_late = keep.tile([P, 12 * P], U32, name="words_late", tag="slot_words", align_bytes=64)
+        gather(scales_late, 0, 14, 4, scale_window, slot_scales)
+        gather(words_late, 0, 12, 4, word_window, slot_words)
+        gather(scales_late, 4, 10, 4, scale_window, slot_scales)
+        gather(words_late, 4, 10, 2, word_window, slot_words)
+        gather(scales_late, 8, 0, 4, scale_window, slot_scales)
+        gather(words_late, 6, 0, 2, word_window, slot_words)
+        gather(words_late, 8, 2, 4, word_window, slot_words)
+        gather(scales_late, 12, 4, 2, scale_window, slot_scales)
 
-        for step in range(1, E):
-            waiting = pairs
-            if step < TURNED:
-                pairs = hidden_cold(step, range(BLOCKS))
-            else:
-                hidden_hot(step)
-            if step == 1:
-                turn_cold(0, waiting)
-            if step == 4:
-                turn_cold(1, pairs)
+        for step in WORK[1:]:
+            hidden_hot(step)
+            if step == 5:
+                turn_cold(0, pairs)
 
         for number in (1, 0, 2, 3, 4):
             group = GROUPS[number]

from contextlib import ExitStack

import concourse.mybir as mybir
from concourse.masks import make_identity

K, T, E, C, H, N, HOT, TOP = 512, 768, 9, 256, 512, 128, 3, 3
COLD = E - HOT
S = E * C
FLOPS = 2 * S * (K * H + H * N)

P = 128
PACK = 4
QUADRANTS = 4
QUADRANT = P // QUADRANTS
QUADRANT_ROWS = 4
LIST_ROWS = 16
BLOCKS = C // P

F32 = mybir.dt.float32
BF16 = mybir.dt.bfloat16
I32 = mybir.dt.int32
U32 = mybir.dt.uint32
U16 = mybir.dt.uint16
U8 = mybir.dt.uint8
FP8X4 = mybir.dt.float8_e4m3fn_x4
FP4X4 = mybir.dt.float4_e2m1fn_x4
SILU = mybir.ActivationFunctionType.Silu
MULT = mybir.AluOpType.mult
ADD = mybir.AluOpType.add

ORDER = [3, 4, 7, 8, 5, 6, 0, 1, 2]
WORK = [0, 1, 3, 2, 5, 4, 6, 7, 8]
GROUPS = [(0, 1), (2, 3), (4, 5), (6, 7), (8,)]
TURNED = 2
TURNED_ON_SCALAR = 0
RESULTS_ON_SCALAR = (0, 1, 3)
SHIFTED = 112
RING = 3
LAST_EXPERT_BANKS = (4, 5)
TURN_BANKS = (7,)
RESULT_BANKS = (2, 1, 5, 3, 6)
OWN_BANKS = {9: 7}
TOKEN_CHUNKS = [(0, 384), (384, 512)]
SUMMED_IN_PSUM = 2
BACK_BANKS = (5, 6)


def tile_moe_hot_mlp_silu_kernel(
    tc, x_words, x_scales, w1h_words, w1h_scales, w2h_words, w2h_scales, w1c_words, w1c_scales,
    w2c_words, w2c_scales, gate, offs, pos1, pos2, pos3, out,
):
    nc = tc.nc
    with ExitStack() as ctx:
        keep = ctx.enter_context(tc.tile_pool(name="keep", bufs=1))
        ring = ctx.enter_context(tc.tile_pool(name="ring", bufs=7))
        psum = ctx.enter_context(tc.psum_pool(name="psum", bufs=1))

        offs_sb = keep.tile([P, S // LIST_ROWS], U16, name="offs_sb")
        pos_sb = [keep.tile([P, T // LIST_ROWS], U16, name=f"pos_sb{r}") for r in range(TOP)]
        token_words = keep.tile([P, T], I32, name="token_words", align_bytes=64)
        token_scales = keep.tile([P, T], U8, name="token_scales", align_bytes=64)
        w1c_first = keep.tile([P, TURNED, 2 * H], U8, name="w1c_first", align_bytes=64)
        w1c_raw = keep.tile([P, COLD - TURNED, 2 * H], U8, name="w1c_raw", align_bytes=64)
        w1h_raw = keep.tile([P, HOT, H], I32, name="w1h_raw", align_bytes=64)
        w2c = keep.tile([P, COLD, 2 * N], U8, name="w2c", align_bytes=64)
        w2h = keep.tile([P, HOT, PACK * N], U8, name="w2h", align_bytes=64)
        s1c_first = keep.tile([P, 2, H], U8, name="s1c_first", align_bytes=64)
        s1c_raw = keep.tile([P, H], U8, name="s1c_raw", align_bytes=64)
        s1c_shifted = [
            keep.tile([P, H], U8, name=f"s1c_shifted{a}", align_bytes=64) for a in range(COLD - TURNED - 1)
        ]
        s1h_raw = keep.tile([P, H], U8, name="s1h_raw", align_bytes=64)
        s2c = keep.tile([P, COLD, N], U8, name="s2c", align_bytes=64)
        s2h = keep.tile([P, HOT, N], U8, name="s2h", align_bytes=64)
        gate_sb = keep.tile([P, TOP, T], F32, name="gate_sb")
        y = keep.tile([P, S], F32, name="y")
        ident = keep.tile([P, P], F32, name="ident")
        warm_in = keep.tile([P, 8], F32, name="warm_in")
        warm_out = keep.tile([P, 8], F32, name="warm_out")

        nc.gpsimd.dma_start(
            w1c_first[:].bitcast(I32), w1c_words[:TURNED, 0].rearrange("e p b -> p e b").bitcast(I32)
        )
        nc.vector.memset(warm_in[:], 0.0)
        for plane in (s1c_first, s1c_raw):
            nc.vector.memset(plane[:].bitcast(I32), 0)
        for plane in (s1h_raw, *s1c_shifted, s2c, s2h):
            nc.gpsimd.memset(plane[:].bitcast(I32), 0)
        make_identity(nc, ident[:])

        def load_words(tile, words):
            nc.sync.dma_start(tile[:].bitcast(I32), words.rearrange("e p b -> p e b").bitcast(I32))

        def load_scales(plane, scales, rows=range(QUADRANT_ROWS)):
            for j in rows:
                nc.sync.dma_start(
                    plane[j:P:QUADRANT].bitcast(I32),
                    scales[:, 0, j::QUADRANT_ROWS, :].rearrange("e q i -> q e i").bitcast(I32),
                )

        def load_stacked(plane, scales, place=0):
            for q in range(QUADRANTS):
                nc.sync.dma_start(
                    plane[QUADRANT * q + QUADRANT_ROWS * place :][: scales.shape[0] * QUADRANT_ROWS, :].bitcast(I32),
                    scales[:, 0, QUADRANT_ROWS * q : QUADRANT_ROWS * (q + 1), :].bitcast(I32),
                )

        def permute_columns(dst, src, line):
            nc.gpsimd.tensor_copy(
                dst.rearrange("p (t a m) -> p a t m", t=PACK, m=line),
                src.rearrange("p (a m t) -> p a t m", t=PACK, m=line),
            )

        for q in range(QUADRANTS):
            queue = nc.sync if q < QUADRANTS // 2 else nc.scalar
            rows = x_scales[0, QUADRANT_ROWS * q : QUADRANT_ROWS * (q + 1), :].bitcast(I32)
            queue.dma_start(
                token_scales[QUADRANT * q : QUADRANT * (q + 1), :].bitcast(I32),
                rows.unsqueeze(0).broadcast_to([QUADRANT // QUADRANT_ROWS, QUADRANT_ROWS, T // 4]),
            )
        nc.sync.dma_start(offs_sb[:], offs)
        load_scales(s1c_first, w1c_scales[:: COLD - 1], (0, 1))
        nc.sync.dma_start(token_words[:], x_words[0].rearrange("p t d -> p (t d)").bitcast(I32))
        nc.scalar.activation(warm_out[:], warm_in[:], SILU)
        load_scales(s1c_first, w1c_scales[:: COLD - 1], (2, 3))
        load_stacked(s1c_raw, w1c_scales[1 : COLD - 1])
        load_words(w1c_raw, w1c_words[TURNED:, 0])
        nc.sync.dma_start(w1h_raw[:], w1h_words[:, 0].rearrange("e p i d -> p e (i d)").bitcast(I32))
        load_stacked(s1h_raw, w1h_scales[:2])
        w1c_second = keep.tile([P, 2 * H], U8, name="w1c_second", align_bytes=64)
        permute_columns(w1c_second[:].bitcast(U16), w1c_first[:, 1, :].bitcast(U16), 8)
        s1c_stacked = keep.tile([P, H], U8, name="s1c_stacked", align_bytes=64)
        permute_columns(s1c_stacked[:], s1c_raw[:], 16)
        for a in (3, 2, 1):
            nc.sync.dma_start(
                s1c_shifted[a - 1][:SHIFTED, :].bitcast(I32),
                s1c_stacked[QUADRANT_ROWS * a : QUADRANT_ROWS * a + SHIFTED, :].bitcast(I32),
            )
        load_stacked(s1h_raw, w1h_scales[2:], 2)
        load_words(w2c, w2c_words[:, 0])
        load_scales(s2c, w2c_scales)
        nc.sync.dma_start(gate_sb[:], gate.rearrange("r p t -> p r t"))
        load_words(w2h, w2h_words[:, 0].rearrange("e p n d -> e p (n d)"))
        load_scales(s2h, w2h_scales)
        for r, pos in enumerate((pos1, pos2, pos3)):
            nc.sync.dma_start(pos_sb[r][:], pos)

        def gather(tile, column, first, blocks, window, gathered):
            entries = offs_sb[:, first * P // LIST_ROWS : (first + blocks) * P // LIST_ROWS]
            nc.vector.tensor_copy(tile[:, column * P : (column + blocks) * P], window.indirect(entries))
            for b in range(blocks):
                gathered[first + b] = tile[:, (column + b) * P : (column + b + 1) * P]

        def first_bank(step, b):
            block = WORK.index(step) * BLOCKS + b
            if block in OWN_BANKS:
                return f"bank{OWN_BANKS[block]}"
            return f"bank{block % RING if step < E - 1 else LAST_EXPERT_BANKS[b]}"

        def hidden_cold(step, blocks):
            w1 = w1c_first[:, step, :].bitcast(FP4X4)
            w1_scale = s1c_first[:, step, :]
            pairs = []
            for b in blocks:
                pre = psum.tile([P, H], F32, name="pre", tag=first_bank(step, b))
                nc.tensor.matmul_mx(
                    pre[:],
                    lhsT=slot_words[ORDER[step] * BLOCKS + b].bitcast(FP8X4),
                    lhsT_scale=slot_scales[ORDER[step] * BLOCKS + b],
                    rhs=w1, rhs_scale=w1_scale, start=True, stop=True,
                )
                h = ring.tile([P, H], BF16, name="h")
                nc.scalar.activation(
                    h[:].rearrange("s (u p d) -> s u p d", u=2, d=2),
                    pre[:].rearrange("s (p u d) -> s u p d", u=2, d=2),
                    SILU,
                )
                pairs.append(h[:].bitcast(F32))
            return pairs

        def turn_cold(step, pairs):
            turned = psum.tile([P, BLOCKS, 2, P], F32, name="turned", tag=f"bank{TURN_BANKS[step]}")
            for b in range(BLOCKS):
                for u in range(2):
                    nc.tensor.transpose(turned[:, b, u, :], pairs[b][:, u * P : (u + 1) * P], ident[:])
            copy = nc.scalar.copy if step < TURNED_ON_SCALAR else nc.vector.tensor_copy
            copy(
                hidden[step].bitcast(F32).rearrange("p (b s u) -> p b s u", s=P, u=2),
                turned[:].rearrange("p b u s -> p b s u"),
            )

        def hidden_hot(step):
            w1, w1_scale = permuted[step]
            word = w1.shape[1] // H
            for b in range(BLOCKS):
                pre = psum.tile([P, H], F32, name="pre", tag=first_bank(step, b))
                for t in range(PACK):
                    cols = slice(t * P, (t + 1) * P)
                    nc.tensor.matmul_mx(
                        pre[:, cols],
                        lhsT=w1[:, word * t * P : word * (t + 1) * P].bitcast(FP4X4 if step < COLD else FP8X4),
                        lhsT_scale=w1_scale[:, cols],
                        rhs=slot_words[ORDER[step] * BLOCKS + b].bitcast(FP8X4),
                        rhs_scale=slot_scales[ORDER[step] * BLOCKS + b],
                        start=True, stop=True,
                    )
                nc.scalar.activation(
                    hidden[step][:, b * H : (b + 1) * H].rearrange("p (c s t) -> p c t s", t=PACK, s=2),
                    pre[:].rearrange("p (t c s) -> p c t s", t=PACK, s=2),
                    SILU,
                )

        def second_layer(number, group, h_words, h_scales):
            y_ps = psum.tile([P, len(group) * C], F32, name="y_ps", tag=f"bank{RESULT_BANKS[number]}")
            for place, step in enumerate(group):
                if step < COLD:
                    f = ORDER[step] - HOT
                    w2, w2_scale = w2c[:, f, :].bitcast(FP4X4), s2c[:, f, :]
                else:
                    w2, w2_scale = w2h[:, step - COLD, :].bitcast(FP8X4), s2h[:, step - COLD, :]
                cols = slice(place * C, (place + 1) * C)
                nc.tensor.matmul_mx(
                    y_ps[:, cols], lhsT=w2, lhsT_scale=w2_scale,
                    rhs=h_words[:, cols].bitcast(FP8X4), rhs_scale=h_scales[:, cols], start=True, stop=True,
                )
            first_slot = ORDER[group[0]] * C
            copy = nc.scalar.copy if number in RESULTS_ON_SCALAR else nc.vector.tensor_copy
            copy(y[:, first_slot : first_slot + len(group) * C], y_ps[:])

        scale_window, word_window = token_scales[:], token_words[:].bitcast(U32)
        scales_head = keep.tile([P, P], U8, name="scales_head", tag="slot_scales", align_bytes=64)
        scales_early = keep.tile([P, 3 * P], U8, name="scales_early", align_bytes=64)
        words_head = keep.tile([P, P], U32, name="words_head", tag="slot_words", align_bytes=64)
        words_early = keep.tile([P, 5 * P], U32, name="words_early", align_bytes=64)
        slot_scales, slot_words = {}, {}
        gather(scales_head, 0, 6, 1, scale_window, slot_scales)
        gather(scales_early, 0, 7, 3, scale_window, slot_scales)
        gather(words_head, 0, 6, 1, word_window, slot_words)
        gather(words_early, 0, 7, 3, word_window, slot_words)
        gather(words_early, 3, 16, 2, word_window, slot_words)

        permuted = {1: (w1c_second[:], s1c_stacked[:])}
        for step in WORK[2:]:
            cold = step < COLD
            w1 = keep.tile([P, (2 if cold else PACK) * H], U8, name=f"w1_permuted{step}", align_bytes=64)
            if cold:
                f = ORDER[step] - HOT
                if f == COLD - 1:
                    s1c_last = keep.tile([P, H], U8, name="s1c_last", align_bytes=64)
                    permute_columns(s1c_last[:], s1c_first[:, 1, :], 16)
                permute_columns(w1[:].bitcast(U16), w1c_raw[:, f - TURNED, :].bitcast(U16), 8)
                w1_scale = s1c_last[:] if f == COLD - 1 else s1c_shifted[f - TURNED][:]
            else:
                permute_columns(w1[:].bitcast(I32), w1h_raw[:, step - COLD, :], 4)
                if step == COLD:
                    s1h = keep.tile([P, H], U8, name="s1h", align_bytes=64)
                    permute_columns(s1h[:], s1h_raw[:], 16)
                w1_scale = s1h[QUADRANT_ROWS * (step - COLD) :, :]
            permuted[step] = (w1[:], w1_scale)

        grouped = [
            keep.tile([P, len(group), PACK * C], BF16, name=f"grouped{group[0]}", align_bytes=64) for group in GROUPS
        ]
        hidden = [grouped[step // 2][:, step % 2, :] for step in range(E)]

        pairs = hidden_cold(0, range(BLOCKS))
        scales_late = keep.tile([P, 14 * P], U8, name="scales_late", tag="slot_scales", align_bytes=64)
        words_late = keep.tile([P, 12 * P], U32, name="words_late", tag="slot_words", align_bytes=64)
        gather(scales_late, 0, 14, 4, scale_window, slot_scales)
        gather(words_late, 0, 12, 4, word_window, slot_words)
        gather(scales_late, 4, 10, 4, scale_window, slot_scales)
        gather(words_late, 4, 10, 2, word_window, slot_words)
        gather(scales_late, 8, 0, 4, scale_window, slot_scales)
        gather(words_late, 6, 0, 2, word_window, slot_words)
        gather(words_late, 8, 2, 4, word_window, slot_words)
        gather(scales_late, 12, 4, 2, scale_window, slot_scales)

        for step in WORK[1:]:
            hidden_hot(step)
            if step == 5:
                turn_cold(0, pairs)

        for number in (1, 0, 2, 3, 4):
            group = GROUPS[number]
            h_words = ring.tile([P, len(group) * C], U32, name="h_words", align_bytes=64)
            h_scales = ring.tile([P, len(group) * C], U8, name="h_scales", align_bytes=64)
            nc.vector.quantize_mx(
                h_words[:].bitcast(FP8X4), h_scales[:], grouped[number][:].rearrange("p g x -> p (g x)")
            )
            second_layer(number, group, h_words, h_scales)

        parts = [keep.tile([P, T], F32, name=f"part{r}") for r in range(TOP)]

        def gated(r, lo, hi):
            entries = pos_sb[r][:, lo // LIST_ROWS : hi // LIST_ROWS]
            nc.vector.tensor_tensor(parts[r][:, lo:hi], y[:].indirect(entries), gate_sb[:, r, lo:hi], MULT)

        def sum_in_psum(chunk):
            lo, hi = TOKEN_CHUNKS[chunk]
            sum_sb = keep.tile([P, hi - lo], F32, name=f"sum_sb{chunk}")
            for column in range(lo, hi, P):
                sum_ps = psum.tile([P, P], F32, name="sum_ps", tag=f"bank{column // P}")
                for r in range(TOP):
                    nc.tensor.matmul(
                        sum_ps[:], parts[r][:, column : column + P], ident[:],
                        start=(r == 0), stop=(r == TOP - 1), is_transpose=True,
                    )
                nc.scalar.copy(sum_sb[:, column - lo : column - lo + P], sum_ps[:])
            back_ps = psum.tile([P, hi - lo], F32, name="back_ps", tag=f"bank{BACK_BANKS[chunk]}")
            for column in range(0, hi - lo, P):
                nc.tensor.transpose(back_ps[:, column : column + P], sum_sb[:, column : column + P], ident[:])
            total = keep.tile([P, hi - lo], F32, name=f"total{chunk}")
            nc.scalar.copy(total[:], back_ps[:])
            nc.scalar.dma_start(out[:, lo:hi], total[:])

        first = TOKEN_CHUNKS[-1][1]
        for r in range(TOP - 1):
            gated(r, 0, first)
        for chunk, (lo, hi) in enumerate(TOKEN_CHUNKS):
            gated(TOP - 1, lo, hi)
            sum_in_psum(chunk)
        for r in range(TOP - 1):
            gated(r, first, T)
        pair = keep.tile([P, T - first], F32, name="pair")
        gated(TOP - 1, first, first + P)
        nc.vector.tensor_tensor(pair[:], parts[0][:, first:], parts[1][:, first:], ADD)
        gated(TOP - 1, first + P, T)
        for lo in range(first, T, P):
            total = keep.tile([P, P], F32, name=f"total_last{lo}")
            nc.vector.tensor_tensor(total[:], pair[:, lo - first : lo - first + P], parts[TOP - 1][:, lo : lo + P], ADD)
            nc.sync.dma_start(out[:, lo : lo + P], total[:])
